import numpy as np
import ml_dtypes


def mxq(x, axis, fmt="e4m3"):
    dtype, down = {"e4m3": (ml_dtypes.float8_e4m3fn, 7), "e5m2": (ml_dtypes.float8_e5m2, 14)}[fmt]
    v = np.moveaxis(np.asarray(x, np.float32).astype(ml_dtypes.bfloat16).astype(np.float64), axis, -1)
    blocks = v.reshape(v.shape[:-1] + (-1, 32))
    amax = np.abs(blocks).max(-1, keepdims=True)
    byte = np.maximum(np.where(amax > 0, np.frexp(amax)[1] - 1 + 127, 0) - down, 1)
    scale = np.exp2(byte - 127.0)
    codes = (blocks / scale).astype(np.float32).astype(dtype).astype(np.float64)
    return np.moveaxis((codes * scale).reshape(v.shape), -1, axis)


WIDE = False


def mx_kscale(k):
    if not WIDE:
        return np.ones(k)
    levels = np.array([10, -10, 5, -5, 0])
    if k % 512:
        return np.exp2(np.random.permutation(np.resize(levels, k // 32))).repeat(32)
    a = np.empty((k // 512, 16))
    for p in range(k // 512):
        a[p, :8] = np.random.permutation(np.resize(levels, 8))
        for g in range(8):
            far = levels[np.abs(levels - a[p, g]) >= 10]
            a[p, g + 8] = far[np.random.randint(len(far))]
    return np.exp2(a.ravel()).repeat(32)


BF16 = ml_dtypes.bfloat16


def bf(x):
    return np.asarray(x, np.float32).astype(BF16)


def f64(x):
    return np.asarray(x).astype(np.float64)


E2M1 = np.array([0.0, 0.5, 1.0, 1.5, 2.0, 3.0, 4.0, 6.0, -0.0, -0.5, -1.0, -1.5, -2.0, -3.0, -4.0, -6.0])


def pack_weight(w, fmt):
    k, n = w.shape
    w = f64(bf(w)).reshape(k // 32, 32, n)
    amax = np.abs(w).max(1)
    if fmt == "e4m3":
        byte = np.frexp(amax)[1] - 1 + 127 - 7
    else:
        mant, ex = np.frexp(amax / 6.0)
        byte = np.where(mant > 0.5, ex, ex - 1) + 127
    byte = np.clip(np.where(amax > 0, byte, 1), 1, 254)
    scaled = (w * np.exp2(127.0 - byte)[:, None, :]).reshape(k, n).astype(np.float32)
    by_word = np.ascontiguousarray(scaled.reshape(k // 512, 128, 4, n).transpose(0, 1, 3, 2))
    if fmt == "e4m3":
        words = by_word.astype(ml_dtypes.float8_e4m3fn).view(np.uint8)
    else:
        c = by_word.astype(ml_dtypes.float4_e2m1fn).view(np.uint8) & 0xF
        words = c[..., 0::2] | (c[..., 1::2] << 4)
    return np.ascontiguousarray(words), np.ascontiguousarray(byte.astype(np.uint8).reshape(k // 512, 16, n))


def unpack_weight(words, scales, fmt):
    g, p, n, _ = words.shape
    if fmt == "e4m3":
        vals = np.ascontiguousarray(words).view(ml_dtypes.float8_e4m3fn).astype(np.float64)
    else:
        nib = np.empty((g, p, n, 4), np.uint8)
        nib[..., 0::2] = words & 0xF
        nib[..., 1::2] = words >> 4
        vals = E2M1[nib]
    vals = vals * np.repeat(np.exp2(scales.astype(np.float64) - 127.0), 8, axis=1)[..., None]
    return vals.transpose(0, 1, 3, 2).reshape(g * 512, n)
def pack4(w):
    words, scales = pack_weight(w, "e2m1")
    return words.reshape(words.shape[0], 128, -1), scales


def unpack4(words, scales):
    return unpack_weight(words.reshape(words.shape[0], 128, -1, 2), scales, "e2m1")


G, T, S, V, P = 4, 1024, 512, 1024, 256


def setup_inputs():
    s, t = mx_kscale(G * S), mx_kscale(G * V)
    inv = np.random.standard_normal((G * S, V)) / np.sqrt(S) / s[:, None]
    par = np.abs(np.random.standard_normal((G * V, P))) / np.sqrt(V) / t[:, None]
    inv_words, inv_scales = pack4(inv)
    par_words, par_scales = pack4(par)
    return {"x": bf(np.random.standard_normal((G, T, S)) * s.reshape(G, 1, S)),
            "inv_words": inv_words, "inv_scales": inv_scales,
            "base": bf(1 + 0.1 * np.random.standard_normal((G, V))),
            "ivar": bf((1 + 0.1 * np.random.standard_normal((G, V))) * t.reshape(G, V)),
            "par_words": par_words, "par_scales": par_scales}


def reference(x, inv_words, inv_scales, base, ivar, par_words, par_scales):
    w = unpack4(inv_words, inv_scales).reshape(G, S, V)
    a = unpack4(par_words, par_scales).reshape(G, V, P)
    y = mxq(f64(x), 2, "e4m3") @ w
    z = (np.square(y) - f64(base)[:, None, :]) * f64(ivar)[:, None, :]
    return mxq(z, 2, "e4m3") @ a

@@ -1,0 +1,295 @@
+from contextlib import ExitStack
+
+import concourse.mybir as mybir
+from concourse.masks import make_identity
+
+G, T, S, V, NP = 4, 1024, 512, 1024, 256
+FLOPS = 2 * G * T * S * V + 2 * G * T * V * NP
+
+F32 = mybir.dt.float32
+BF16 = mybir.dt.bfloat16
+I32 = mybir.dt.int32
+U32 = mybir.dt.uint32
+U16 = mybir.dt.uint16
+U8 = mybir.dt.uint8
+FP8X4 = mybir.dt.float8_e4m3fn_x4
+FP4X4 = mybir.dt.float4_e2m1fn_x4
+ACT = mybir.ActivationFunctionType
+ALU = mybir.AluOpType
+
+P = 128
+TOK = 512
+NBLK = G * T // TOK
+NUNIT = 2 * NBLK
+HALF = TOK // 2
+HALVED = (0, NUNIT - 1)
+
+
+def tile_eeg_band_parcel_power_s14_kernel(tc, x, inv_words, inv_scales, base, ivar, par_words, par_scales, out):
+    nc = tc.nc
+    with ExitStack() as ctx:
+        sb = ctx.enter_context(tc.tile_pool(name="sb", bufs=1))
+        ps = ctx.enter_context(tc.psum_pool(name="ps", bufs=1))
+        ctx.enter_context(tc.manual_schedule())
+
+        def ring(pool, name, count, shape, dtype):
+            return [pool.tile(shape, dtype, name="%s%d" % (name, i), align_bytes=64) for i in range(count)]
+
+        def banks(name, count, shape):
+            return [ps.tile(shape, F32, name="%s%d" % (name, i)) for i in range(count)]
+
+        ident = sb.tile([P, P], F32, name="ident", align_bytes=64)
+        warm = sb.tile([P, 8], F32, name="warm", align_bytes=64)
+        warm_out = sb.tile([P, 8], F32, name="warm_out", align_bytes=64)
+        x_sb = ring(sb, "x", 2 * NBLK, [P, 2 * S], BF16)
+        inv_raw = ring(sb, "invraw", G, [P, 2 * V], U8)
+        inv_w = ring(sb, "invw", G, [P, 2 * V], U8)
+        invs_raw = sb.tile([P, G, V], U8, name="invs_raw", align_bytes=64)
+        inv_s = ring(sb, "invs", G, [P, V], U8)
+        par_w = sb.tile([P, 2 * G, 2 * NP], U8, name="par_w", align_bytes=64)
+        par_s = sb.tile([P, 2 * G, NP], U8, name="par_s", align_bytes=64)
+        base_sb = sb.tile([P, 2 * G, 4], BF16, name="base_sb", align_bytes=64)
+        ivar_sb = sb.tile([P, 2 * G, 4], BF16, name="ivar_sb", align_bytes=64)
+        xg = ring(sb, "xg", 3, [P, 4 * TOK], BF16)
+        xq = ring(sb, "xq", 3, [P, TOK], U32)
+        xs = ring(sb, "xs", 3, [P, TOK], U8)
+        sq_sb = ring(sb, "sq", 3, [P, 4, TOK], F32)
+        z_sep = ring(sb, "zsep", 3, [P, 4, TOK], BF16)
+        z_int = ring(sb, "zint", 3, [P, 4 * TOK], BF16)
+        zq = ring(sb, "zq", 8, [P, TOK], U32)
+        zs = ring(sb, "zs", 8, [P, TOK], U8)
+        res = ring(sb, "res", NUNIT, [P, 2 * NP], F32)
+        y_ps = banks("y", 4, [P, TOK])
+        xt_ps = banks("xt", 2, [P, 2, 2, P])
+        o_ps = banks("o", 2, [P, 2, NP])
+
+        x_rows = x.rearrange("g (j p a i) s -> g j a p (i s)", j=2, p=P, a=2, i=2)
+        out_rows = out.rearrange("g (j p a i) c -> g j a p (i c)", j=2, p=P, a=2, i=2)
+
+        def load_x(m):
+            b, a = divmod(m, 2)
+            nc.sync.dma_start(out=x_sb[m][:], in_=x_rows[b // 2, b % 2, a])
+
+        def load_inv(g):
+            nc.sync.dma_start(out=inv_raw[g][:].bitcast(I32), in_=inv_words[g].bitcast(I32))
+
+        def load_scales(queue, plane, src):
+            for q in range(4):
+                queue.dma_start(
+                    out=plane[32 * q : 32 * q + 4, :, :].bitcast(I32),
+                    in_=src[:, 4 * q : 4 * q + 4, :].rearrange("g r n -> r g n").bitcast(I32),
+                )
+
+        def deal_words(g):
+            nc.vector.tensor_copy(
+                out=inv_w[g][:].bitcast(U16).rearrange("p (h t m) -> p h t m", h=2, t=4),
+                in_=inv_raw[g][:].bitcast(U16).rearrange("p (h m t) -> p h t m", h=2, t=4),
+            )
+
+        def deal_scales(g):
+            nc.vector.tensor_copy(
+                out=inv_s[g][:].rearrange("p (h t m) -> p h t m", h=2, t=4),
+                in_=invs_raw[:, g, :].rearrange("p (h m t) -> p h t m", h=2, t=4),
+            )
+
+        def transpose_x(m):
+            words = x_sb[m][:].bitcast(F32)
+            for i in range(2):
+                for u in range(2):
+                    nc.tensor.transpose(xt_ps[m % 2][:, i, u, :], words[:, 256 * i + u : 256 * (i + 1) : 2], ident[:])
+
+        def copy_x(m, on_vector=False):
+            b, a = divmod(m, 2)
+            dst = xg[b % 3][:, a * 2 * TOK : (a + 1) * 2 * TOK].bitcast(F32).rearrange("p (i r u) -> p i r u", i=2, u=2)
+            src = xt_ps[m % 2][:].rearrange("p i u r -> p i r u")
+            if on_vector:
+                nc.vector.tensor_copy(out=dst, in_=src)
+            else:
+                nc.scalar.copy(out=dst, in_=src)
+
+        def quant_x(b, lo=0, hi=TOK):
+            nc.vector.quantize_mx(
+                out=xq[b % 3][:, lo:hi].bitcast(FP8X4), scales=xs[b % 3][:, lo:hi], in_=xg[b % 3][:, 4 * lo : 4 * hi]
+            )
+
+        def mm1_cols(n, t, dst, lo, hi):
+            b, h = divmod(n, 2)
+            g, col = b // 2, P * (4 * h + t)
+            nc.tensor.matmul_mx(
+                out=dst,
+                lhsT=inv_w[g][:, 2 * col : 2 * (col + P)].bitcast(FP4X4),
+                lhsT_scale=inv_s[g][:, col : col + P],
+                rhs=xq[b % 3][:, lo:hi].bitcast(FP8X4),
+                rhs_scale=xs[b % 3][:, lo:hi],
+                start=True,
+                stop=True,
+            )
+
+        def mm1(n, k):
+            if n in HALVED:
+                a, t0 = k // 2, 2 * (k % 2)
+                for e in range(2):
+                    mm1_cols(n, t0 + e, y_ps[k][:, HALF * e : HALF * (e + 1)], HALF * a, HALF * (a + 1))
+            else:
+                mm1_cols(n, k, y_ps[k][:], 0, TOK)
+
+        def square(n, k):
+            if n in HALVED:
+                a, t0 = k // 2, 2 * (k % 2)
+                dst = sq_sb[n % 3][:, t0 : t0 + 2, HALF * a : HALF * (a + 1)]
+                src = y_ps[k][:].rearrange("p (e c) -> p e c", e=2)
+            else:
+                dst, src = sq_sb[n % 3][:, k, :], y_ps[k][:]
+            nc.scalar.activation(out=dst, in_=src, func=ACT.Square)
+
+        def affine(n, t, lo=0, hi=TOK):
+            b, h = divmod(n, 2)
+            gh = 2 * (b // 2) + h
+            nc.vector.tensor_scalar(
+                out=z_sep[n % 3][:, t, lo:hi],
+                in0=sq_sb[n % 3][:, t, lo:hi],
+                scalar1=base_sb[:, gh, t : t + 1],
+                scalar2=ivar_sb[:, gh, t : t + 1],
+                op0=ALU.subtract,
+                op1=ALU.mult,
+            )
+
+        def interleave(n, lo, hi):
+            nc.vector.tensor_copy(
+                out=z_int[n % 3][:, 4 * lo : 4 * hi].rearrange("p (c i t) -> p c t i", i=4, t=4),
+                in_=z_sep[n % 3][:, :, lo:hi].rearrange("p t (c i) -> p c t i", i=4),
+            )
+
+        def quant_z(n, lo, hi):
+            nc.vector.quantize_mx(
+                out=zq[n % 8][:, lo:hi].bitcast(FP8X4), scales=zs[n % 8][:, lo:hi], in_=z_int[n % 3][:, 4 * lo : 4 * hi]
+            )
+
+        def mm2_tile(m, i, dst):
+            b, a = divmod(m, 2)
+            g = b // 2
+            cols = slice(P * (2 * a + i), P * (2 * a + i + 1))
+            for c in range(2):
+                for h in range(2):
+                    n = 2 * b + h
+                    nc.tensor.matmul_mx(
+                        out=dst[:, P * c : P * (c + 1)],
+                        lhsT=zq[n % 8][:, cols].bitcast(FP8X4),
+                        lhsT_scale=zs[n % 8][:, cols],
+                        rhs=par_w[:, 2 * g + h, 256 * c : 256 * (c + 1)].bitcast(FP4X4),
+                        rhs_scale=par_s[:, 2 * g + h, P * c : P * (c + 1)],
+                        start=(h == 0),
+                        stop=(h == 1),
+                    )
+
+        def mm2(m):
+            for i in range(2):
+                mm2_tile(m, i, o_ps[m % 2][:, i, :])
+
+        def finish(m):
+            b, a = divmod(m, 2)
+            nc.scalar.copy(out=res[m][:], in_=o_ps[m % 2][:].rearrange("p i c -> p (i c)"))
+            nc.sync.dma_start(out=out_rows[b // 2, b % 2, a], in_=res[m][:])
+
+        nc.vector.memset(invs_raw[:].rearrange("p g n -> p (g n)").bitcast(I32), 0)
+        nc.vector.memset(warm[:], 0.0)
+        nc.vector.memset(par_s[:].rearrange("p g n -> p (g n)").bitcast(I32), 0)
+        load_scales(nc.scalar, invs_raw, inv_scales)
+        nc.scalar.activation(out=warm_out[:], in_=warm[:], func=ACT.Square)
+        make_identity(nc, ident[:])
+        load_x(0)
+        load_inv(0)
+        load_x(1)
+        load_x(2)
+        load_x(3)
+        nc.sync.dma_start(out=base_sb[:], in_=base.rearrange("g (h p t) -> p (g h) t", h=2, t=4))
+        nc.sync.dma_start(out=ivar_sb[:], in_=ivar.rearrange("g (h p t) -> p (g h) t", h=2, t=4))
+        load_inv(1)
+        load_inv(2)
+        load_x(4)
+        load_x(5)
+        load_scales(nc.sync, par_s, par_scales)
+        nc.sync.dma_start(out=par_w[:].bitcast(I32), in_=par_words.rearrange("g p n -> p g n").bitcast(I32))
+        load_inv(3)
+        for m in range(6, 2 * NBLK):
+            load_x(m)
+
+        transpose_x(0)
+        transpose_x(1)
+        copy_x(0)
+        copy_x(1)
+        deal_words(0)
+        deal_scales(0)
+        quant_x(0, 0, HALF)
+        quant_x(0, HALF, TOK)
+        mm1(0, 0)
+        mm1(0, 1)
+        transpose_x(2)
+        mm1(0, 2)
+        mm1(0, 3)
+        transpose_x(3)
+        deal_words(1)
+        deal_scales(1)
+
+        F_LAG = 4
+        last = NUNIT - 1
+        for n in range(last):
+            copies = [2, 3] if n == 0 else [4, 5] if n == 1 else [n + 4] if n + 4 < NUNIT else []
+            nxt = [4, 5] if n == 0 else [n + 5] if n + 5 < NUNIT else []
+            for t in range(4):
+                square(n, t)
+                mm1(n + 1, t)
+                if n > 0:
+                    affine(n, t)
+                if t == 1:
+                    if n > 0:
+                        interleave(n - 1, 0, TOK)
+                    if n % 2 == 0 and n >= 2 and n // 2 + 1 < NBLK:
+                        quant_x(n // 2 + 1)
+                    if n >= F_LAG:
+                        mm2(n - F_LAG)
+            if n == 0:
+                deal_words(2)
+                for t in range(4):
+                    affine(0, t)
+            else:
+                quant_z(n - 1, 0, TOK)
+            for m in copies:
+                copy_x(m)
+            if n == 0:
+                quant_x(1)
+            if n == 2:
+                deal_scales(2)
+            if n == 4:
+                deal_words(3)
+            if n == 6:
+                deal_scales(3)
+            if n >= F_LAG:
+                finish(n - F_LAG)
+            for m in nxt:
+                transpose_x(m)
+
+        for k in range(4):
+            square(last, k)
+        interleave(last - 1, 0, TOK)
+        for t in range(4):
+            affine(last, t, 0, HALF)
+        quant_z(last - 1, 0, TOK)
+        interleave(last, 0, HALF)
+        for t in range(4):
+            affine(last, t, HALF, TOK)
+        quant_z(last, 0, HALF)
+        interleave(last, HALF, TOK)
+        for m in range(last - F_LAG, last - 1):
+            mm2(m)
+            finish(m)
+        quant_z(last, HALF, TOK)
+        mm2(last - 1)
+        finish(last - 1)
+        dst = out_rows[G - 1, 1, 1]
+        mm2_tile(last, 0, y_ps[0][:, 0:NP])
+        mm2_tile(last, 1, y_ps[1][:, 0:NP])
+        nc.vector.tensor_copy(out=res[last][:, 0:NP], in_=y_ps[0][:, 0:NP])
+        nc.sync.dma_start(out=dst[:, 0:NP], in_=res[last][:, 0:NP])
+        nc.scalar.copy(out=res[last][:, NP : 2 * NP], in_=y_ps[1][:, 0:NP])
+        nc.scalar.dma_start(out=dst[:, NP : 2 * NP], in_=res[last][:, NP : 2 * NP])

@@ -18,11 +18,52 @@ ACT = mybir.ActivationFunctionType
 ALU = mybir.AluOpType
 
 P = 128
-TOK = 512
-NBLK = G * T // TOK
-NUNIT = 2 * NBLK
-HALF = TOK // 2
-HALVED = (0, NUNIT - 1)
+BANK = 512
+QUARTER = 256
+NSTEP = 16
+NY = 5
+NAUX = 3
+WIDE = ()
+COPY_STEP = [0,0,1,2]+[2 * m - 5 for m in range(4,16)]
+QX_STEP = [0,2]+[4 * b - 3 for b in range(2,8)]
+FIN_STEP = [2 * m + 12 for m in range(16)]
+DEAL_STEP = [-1,0]
+S_AFF = ()
+SPLIT = False
+RUN = 4
+V_COPY = (2,)
+LEAD_O = 2
+HEADFINE = True
+
+
+def step_plan(n):
+    g, s = divmod(n, 4)
+    if n in WIDE:
+        h, t0 = s // 2, 2 * (s % 2)
+        banks = [(g, h, t0 + e, 1, BANK * j, BANK) for e in range(2) for j in range(2)]
+        affs = [[], [(g, h, t0, 0, T)], [], [(g, h, t0 + 1, 0, T)]]
+        done = []
+        if s % 2 == 1:
+            done = [(g, h, 0, BANK), (g, h, BANK, T)] if SPLIT else [(g, h, 0, T)]
+        return banks, affs, done
+    if 4 * g in WIDE:
+        h, j = 1, s - 2
+    else:
+        j, h = divmod(s, 2)
+    lo = BANK * j
+    if n == 0:
+        banks = [(g, h, 2 * e, 2, lo + QUARTER * a, QUARTER) for a in range(2) for e in range(2)]
+        affs = [[(g, h, 2 * e + i, lo + QUARTER * a, lo + QUARTER * (a + 1)) for i in range(2)] for a in range(2) for e in range(2)]
+        if not HEADFINE:
+            affs = [[], [], [(g, h, t, lo, lo + BANK) for t in (0, 1)], [(g, h, t, lo, lo + BANK) for t in (2, 3)]]
+        return banks, affs, [(g, h, lo, lo + BANK)]
+    if n == NSTEP - 1:
+        banks = [(g, h, 2 * e, 2, lo + QUARTER * a, QUARTER) for a in range(2) for e in range(2)]
+        affs = [[(g, h, 2 * e + i, lo + QUARTER * a, lo + QUARTER * (a + 1)) for i in range(2)] for a in range(2) for e in range(2)]
+        return banks, affs, []
+    banks = [(g, h, t, 1, lo, BANK) for t in range(4)]
+    affs = [[(g, h, t, lo, lo + BANK)] for t in range(4)]
+    return banks, affs, [(g, h, lo, lo + BANK)]
 
 
 def tile_eeg_band_parcel_power_s14_kernel(tc, x, inv_words, inv_scales, base, ivar, par_words, par_scales, out):
@@ -32,43 +73,46 @@ def tile_eeg_band_parcel_power_s14_kernel(tc, x, inv_words, inv_scales, base, iv
         ps = ctx.enter_context(tc.psum_pool(name="ps", bufs=1))
         ctx.enter_context(tc.manual_schedule())
 
-        def ring(pool, name, count, shape, dtype):
-            return [pool.tile(shape, dtype, name="%s%d" % (name, i), align_bytes=64) for i in range(count)]
 
-        def banks(name, count, shape):
-            return [ps.tile(shape, F32, name="%s%d" % (name, i)) for i in range(count)]
+        def ring(name, count, shape, dtype):
+            return [sb.tile(shape, dtype, name="%s%d" % (name, i), align_bytes=64) for i in range(count)]
 
         ident = sb.tile([P, P], F32, name="ident", align_bytes=64)
         warm = sb.tile([P, 8], F32, name="warm", align_bytes=64)
         warm_out = sb.tile([P, 8], F32, name="warm_out", align_bytes=64)
-        x_sb = ring(sb, "x", 2 * NBLK, [P, 2 * S], BF16)
-        inv_raw = ring(sb, "invraw", G, [P, 2 * V], U8)
-        inv_w = ring(sb, "invw", G, [P, 2 * V], U8)
-        invs_raw = sb.tile([P, G, V], U8, name="invs_raw", align_bytes=64)
-        inv_s = ring(sb, "invs", G, [P, V], U8)
+        x_sb = ring("x", NSTEP, [P, 2 * S], BF16)
+        inv_raw = ring("invraw", G, [P, 2 * V], U8)
+        inv_w = ring("invw", G, [P, 2 * V], U8)
+        invs_raw = sb.tile([P, V], U8, name="invs_raw", align_bytes=64)
+        inv_s = ring("invs", G, [P, V], U8)
         par_w = sb.tile([P, 2 * G, 2 * NP], U8, name="par_w", align_bytes=64)
         par_s = sb.tile([P, 2 * G, NP], U8, name="par_s", align_bytes=64)
         base_sb = sb.tile([P, 2 * G, 4], BF16, name="base_sb", align_bytes=64)
         ivar_sb = sb.tile([P, 2 * G, 4], BF16, name="ivar_sb", align_bytes=64)
-        xg = ring(sb, "xg", 3, [P, 4 * TOK], BF16)
-        xq = ring(sb, "xq", 3, [P, TOK], U32)
-        xs = ring(sb, "xs", 3, [P, TOK], U8)
-        sq_sb = ring(sb, "sq", 3, [P, 4, TOK], F32)
-        z_sep = ring(sb, "zsep", 3, [P, 4, TOK], BF16)
-        z_int = ring(sb, "zint", 3, [P, 4 * TOK], BF16)
-        zq = ring(sb, "zq", 8, [P, TOK], U32)
-        zs = ring(sb, "zs", 8, [P, TOK], U8)
-        res = ring(sb, "res", NUNIT, [P, 2 * NP], F32)
-        y_ps = banks("y", 4, [P, TOK])
-        xt_ps = banks("xt", 2, [P, 2, 2, P])
-        o_ps = banks("o", 2, [P, 2, NP])
+        gain = sb.tile([P, 2 * G, 4], F32, name="gain", align_bytes=64)
+        shift = sb.tile([P, 2 * G, 4], F32, name="shift", align_bytes=64)
+        xg = ring("xg", 2, [P, 4 * T], BF16)
+        xq = ring("xq", G, [P, T], U32)
+        xs = ring("xs", G, [P, T], U8)
+        sq_sb = ring("sq", 3, [P, 4, T], F32)
+        z_sep = ring("zsep", 2, [P, 4, T], BF16)
+        z_int = ring("zint", 2, [P, 4 * T], BF16)
+        zq = ring("zq", 4, [P, T], U32)
+        zs = ring("zs", 4, [P, T], U8)
+        res = ring("res", 8, [P, 2 * NP], F32)
+        y_ps = [ps.tile([P, BANK], F32, name="y%d" % i) for i in range(NY)]
+        aux_ps = [ps.tile([P, BANK], F32, name="aux%d" % i) for i in range(NAUX)]
+        aux_of = {}
 
-        x_rows = x.rearrange("g (j p a i) s -> g j a p (i s)", j=2, p=P, a=2, i=2)
-        out_rows = out.rearrange("g (j p a i) c -> g j a p (i c)", j=2, p=P, a=2, i=2)
+        def take_aux(key):
+            aux_of[key] = aux_ps[len(aux_of) % NAUX]
+            return aux_of[key]
+
+        x_rows = x.rearrange("g (q p i) s -> g q p (i s)", q=4, p=P, i=2)
+        out_rows = out.rearrange("g (q p i) c -> g q p (i c)", q=4, p=P, i=2)
 
         def load_x(m):
-            b, a = divmod(m, 2)
-            nc.sync.dma_start(out=x_sb[m][:], in_=x_rows[b // 2, b % 2, a])
+            nc.sync.dma_start(out=x_sb[m][:], in_=x_rows[m // 4, m % 4])
 
         def load_inv(g):
             nc.sync.dma_start(out=inv_raw[g][:].bitcast(I32), in_=inv_words[g].bitcast(I32))
@@ -86,210 +130,267 @@ def tile_eeg_band_parcel_power_s14_kernel(tc, x, inv_words, inv_scales, base, iv
                 in_=inv_raw[g][:].bitcast(U16).rearrange("p (h m t) -> p h t m", h=2, t=4),
             )
 
-        def deal_scales(g):
+        def deal_scales():
             nc.vector.tensor_copy(
-                out=inv_s[g][:].rearrange("p (h t m) -> p h t m", h=2, t=4),
-                in_=invs_raw[:, g, :].rearrange("p (h m t) -> p h t m", h=2, t=4),
+                out=inv_s[0][:].rearrange("p (h t m) -> p h t m", h=2, t=4),
+                in_=invs_raw[:].rearrange("p (h m t) -> p h t m", h=2, t=4),
             )
+
+        def shift_scales(g):
+            for q in range(4):
+                nc.sync.dma_start(
+                    out=inv_s[g][32 * q : 32 * q + 4, :].bitcast(I32),
+                    in_=inv_s[0][32 * q + 4 * g : 32 * q + 4 * g + 4, :].bitcast(I32),
+                )
 
         def transpose_x(m):
             words = x_sb[m][:].bitcast(F32)
+            bank = take_aux(("x", m))
             for i in range(2):
                 for u in range(2):
-                    nc.tensor.transpose(xt_ps[m % 2][:, i, u, :], words[:, 256 * i + u : 256 * (i + 1) : 2], ident[:])
+                    c = P * (2 * i + u)
+                    nc.tensor.transpose(bank[:, c : c + P], words[:, 256 * i + u : 256 * (i + 1) : 2], ident[:])
 
-        def copy_x(m, on_vector=False):
-            b, a = divmod(m, 2)
-            dst = xg[b % 3][:, a * 2 * TOK : (a + 1) * 2 * TOK].bitcast(F32).rearrange("p (i r u) -> p i r u", i=2, u=2)
-            src = xt_ps[m % 2][:].rearrange("p i u r -> p i r u")
-            if on_vector:
-                nc.vector.tensor_copy(out=dst, in_=src)
-            else:
-                nc.scalar.copy(out=dst, in_=src)
+        def copy_x(m):
+            copy = nc.vector.tensor_copy if m in V_COPY else nc.scalar.copy
+            g, q = divmod(m, 4)
+            dst = xg[g % 2][:, 4 * QUARTER * q : 4 * QUARTER * (q + 1)].bitcast(F32)
+            copy(
+                out=dst.rearrange("p (i r u) -> p i r u", i=2, u=2),
+                in_=aux_of[("x", m)][:].rearrange("p (i u r) -> p i r u", i=2, u=2),
+            )
 
-        def quant_x(b, lo=0, hi=TOK):
+        def quant_x(g, lo, hi):
             nc.vector.quantize_mx(
-                out=xq[b % 3][:, lo:hi].bitcast(FP8X4), scales=xs[b % 3][:, lo:hi], in_=xg[b % 3][:, 4 * lo : 4 * hi]
+                out=xq[g][:, lo:hi].bitcast(FP8X4), scales=xs[g][:, lo:hi], in_=xg[g % 2][:, 4 * lo : 4 * hi]
             )
 
-        def mm1_cols(n, t, dst, lo, hi):
-            b, h = divmod(n, 2)
-            g, col = b // 2, P * (4 * h + t)
-            nc.tensor.matmul_mx(
-                out=dst,
-                lhsT=inv_w[g][:, 2 * col : 2 * (col + P)].bitcast(FP4X4),
-                lhsT_scale=inv_s[g][:, col : col + P],
-                rhs=xq[b % 3][:, lo:hi].bitcast(FP8X4),
-                rhs_scale=xs[b % 3][:, lo:hi],
-                start=True,
-                stop=True,
+        def mm1(k, bank):
+            g, h, t0, nt, lo, width = bank
+            for e in range(nt):
+                col = P * (4 * h + t0 + e)
+                nc.tensor.matmul_mx(
+                    out=y_ps[k % NY][:, width * e : width * (e + 1)],
+                    lhsT=inv_w[g][:, 2 * col : 2 * (col + P)].bitcast(FP4X4),
+                    lhsT_scale=inv_s[g][:, col : col + P],
+                    rhs=xq[g][:, lo : lo + width].bitcast(FP8X4),
+                    rhs_scale=xs[g][:, lo : lo + width],
+                    start=True,
+                    stop=True,
+                )
+
+        def square(k, bank):
+            g, h, t0, nt, lo, width = bank
+            nc.scalar.activation(
+                out=sq_sb[(2 * g + h) % 3][:, t0 : t0 + nt, lo : lo + width],
+                in_=y_ps[k % NY][:].rearrange("p (e c) -> p e c", e=nt),
+                func=ACT.Square,
             )
 
-        def mm1(n, k):
-            if n in HALVED:
-                a, t0 = k // 2, 2 * (k % 2)
-                for e in range(2):
-                    mm1_cols(n, t0 + e, y_ps[k][:, HALF * e : HALF * (e + 1)], HALF * a, HALF * (a + 1))
+        def affine(g, h, t, lo, hi, on_scalar):
+            u = 2 * g + h
+            dst, src = z_sep[u % 2][:, t, lo:hi], sq_sb[u % 3][:, t, lo:hi]
+            if on_scalar:
+                nc.scalar.activation(
+                    out=dst, in_=src, func=ACT.Identity, scale=gain[:, u, t : t + 1], bias=shift[:, u, t : t + 1]
+                )
             else:
-                mm1_cols(n, k, y_ps[k][:], 0, TOK)
+                nc.vector.tensor_scalar(
+                    out=dst,
+                    in0=src,
+                    scalar1=base_sb[:, u, t : t + 1],
+                    scalar2=ivar_sb[:, u, t : t + 1],
+                    op0=ALU.subtract,
+                    op1=ALU.mult,
+                )
 
-        def square(n, k):
-            if n in HALVED:
-                a, t0 = k // 2, 2 * (k % 2)
-                dst = sq_sb[n % 3][:, t0 : t0 + 2, HALF * a : HALF * (a + 1)]
-                src = y_ps[k][:].rearrange("p (e c) -> p e c", e=2)
-            else:
-                dst, src = sq_sb[n % 3][:, k, :], y_ps[k][:]
-            nc.scalar.activation(out=dst, in_=src, func=ACT.Square)
-
-        def affine(n, t, lo=0, hi=TOK):
-            b, h = divmod(n, 2)
-            gh = 2 * (b // 2) + h
-            nc.vector.tensor_scalar(
-                out=z_sep[n % 3][:, t, lo:hi],
-                in0=sq_sb[n % 3][:, t, lo:hi],
-                scalar1=base_sb[:, gh, t : t + 1],
-                scalar2=ivar_sb[:, gh, t : t + 1],
-                op0=ALU.subtract,
-                op1=ALU.mult,
-            )
-
-        def interleave(n, lo, hi):
+        def interleave(g, h, lo, hi):
+            u = 2 * g + h
             nc.vector.tensor_copy(
-                out=z_int[n % 3][:, 4 * lo : 4 * hi].rearrange("p (c i t) -> p c t i", i=4, t=4),
-                in_=z_sep[n % 3][:, :, lo:hi].rearrange("p t (c i) -> p c t i", i=4),
+                out=z_int[u % 2][:, 4 * lo : 4 * hi].rearrange("p (c i t) -> p c t i", i=RUN, t=4),
+                in_=z_sep[u % 2][:, :, lo:hi].rearrange("p t (c i) -> p c t i", i=RUN),
             )
 
-        def quant_z(n, lo, hi):
+        def quant_z(g, h, lo, hi):
+            u = 2 * g + h
             nc.vector.quantize_mx(
-                out=zq[n % 8][:, lo:hi].bitcast(FP8X4), scales=zs[n % 8][:, lo:hi], in_=z_int[n % 3][:, 4 * lo : 4 * hi]
+                out=zq[u % 4][:, lo:hi].bitcast(FP8X4), scales=zs[u % 4][:, lo:hi], in_=z_int[u % 2][:, 4 * lo : 4 * hi]
             )
 
         def mm2_tile(m, i, dst):
-            b, a = divmod(m, 2)
-            g = b // 2
-            cols = slice(P * (2 * a + i), P * (2 * a + i + 1))
+            g, q = divmod(m, 4)
+            cols = slice(P * (2 * q + i), P * (2 * q + i + 1))
             for c in range(2):
                 for h in range(2):
-                    n = 2 * b + h
+                    u = 2 * g + h
                     nc.tensor.matmul_mx(
                         out=dst[:, P * c : P * (c + 1)],
-                        lhsT=zq[n % 8][:, cols].bitcast(FP8X4),
-                        lhsT_scale=zs[n % 8][:, cols],
-                        rhs=par_w[:, 2 * g + h, 256 * c : 256 * (c + 1)].bitcast(FP4X4),
-                        rhs_scale=par_s[:, 2 * g + h, P * c : P * (c + 1)],
+                        lhsT=zq[u % 4][:, cols].bitcast(FP8X4),
+                        lhsT_scale=zs[u % 4][:, cols],
+                        rhs=par_w[:, u, 2 * P * c : 2 * P * (c + 1)].bitcast(FP4X4),
+                        rhs_scale=par_s[:, u, P * c : P * (c + 1)],
                         start=(h == 0),
                         stop=(h == 1),
                     )
 
         def mm2(m):
+            bank = take_aux(("o", m))
             for i in range(2):
-                mm2_tile(m, i, o_ps[m % 2][:, i, :])
+                mm2_tile(m, i, bank[:, NP * i : NP * (i + 1)])
 
-        def finish(m):
-            b, a = divmod(m, 2)
-            nc.scalar.copy(out=res[m][:], in_=o_ps[m % 2][:].rearrange("p i c -> p (i c)"))
-            nc.sync.dma_start(out=out_rows[b // 2, b % 2, a], in_=res[m][:])
+        def finish(m, on_vector=False):
+            if on_vector:
+                nc.vector.tensor_copy(out=res[m % 8][:], in_=aux_of[("o", m)][:])
+            else:
+                nc.scalar.copy(out=res[m % 8][:], in_=aux_of[("o", m)][:])
+            nc.sync.dma_start(out=out_rows[m // 4, m % 4], in_=res[m % 8][:])
 
-        nc.vector.memset(invs_raw[:].rearrange("p g n -> p (g n)").bitcast(I32), 0)
+        nc.vector.memset(invs_raw[:].bitcast(I32), 0)
         nc.vector.memset(warm[:], 0.0)
+        for g in range(1, G):
+            nc.vector.memset(inv_s[g][:].bitcast(I32), 0)
         nc.vector.memset(par_s[:].rearrange("p g n -> p (g n)").bitcast(I32), 0)
-        load_scales(nc.scalar, invs_raw, inv_scales)
+        for q in range(4):
+            nc.scalar.dma_start(
+                out=invs_raw[32 * q : 32 * q + 16, :].bitcast(I32), in_=inv_scales[:, 4 * q : 4 * q + 4, :].bitcast(I32)
+            )
         nc.scalar.activation(out=warm_out[:], in_=warm[:], func=ACT.Square)
         make_identity(nc, ident[:])
         load_x(0)
         load_inv(0)
         load_x(1)
-        load_x(2)
-        load_x(3)
+        load_inv(1)
         nc.sync.dma_start(out=base_sb[:], in_=base.rearrange("g (h p t) -> p (g h) t", h=2, t=4))
         nc.sync.dma_start(out=ivar_sb[:], in_=ivar.rearrange("g (h p t) -> p (g h) t", h=2, t=4))
-        load_inv(1)
+        load_x(2)
         load_inv(2)
+        load_x(3)
+        load_inv(3)
         load_x(4)
         load_x(5)
-        load_scales(nc.sync, par_s, par_scales)
-        nc.sync.dma_start(out=par_w[:].bitcast(I32), in_=par_words.rearrange("g p n -> p g n").bitcast(I32))
-        load_inv(3)
-        for m in range(6, 2 * NBLK):
-            load_x(m)
+
+        plans = [step_plan(n) for n in range(NSTEP)]
+        all_banks = [bank for plan in plans for bank in plan[0]]
+        deals = [(deal_words, g) for g in range(2, G)]
 
         transpose_x(0)
         transpose_x(1)
         copy_x(0)
         copy_x(1)
         deal_words(0)
-        deal_scales(0)
-        quant_x(0, 0, HALF)
-        quant_x(0, HALF, TOK)
-        mm1(0, 0)
-        mm1(0, 1)
-        transpose_x(2)
-        mm1(0, 2)
-        mm1(0, 3)
-        transpose_x(3)
+        deal_scales()
+        quant_x(0, 0, QUARTER)
         deal_words(1)
-        deal_scales(1)
+        quant_x(0, QUARTER, BANK)
+        quantised = [True] + [False] * (2 * G - 1)
+        issued = [0]
 
-        F_LAG = 4
-        last = NUNIT - 1
-        for n in range(last):
-            copies = [2, 3] if n == 0 else [4, 5] if n == 1 else [n + 4] if n + 4 < NUNIT else []
-            nxt = [4, 5] if n == 0 else [n + 5] if n + 5 < NUNIT else []
-            for t in range(4):
-                square(n, t)
-                mm1(n + 1, t)
-                if n > 0:
-                    affine(n, t)
-                if t == 1:
-                    if n > 0:
-                        interleave(n - 1, 0, TOK)
-                    if n % 2 == 0 and n >= 2 and n // 2 + 1 < NBLK:
-                        quant_x(n // 2 + 1)
-                    if n >= F_LAG:
-                        mm2(n - F_LAG)
-            if n == 0:
-                deal_words(2)
-                for t in range(4):
-                    affine(0, t)
-            else:
-                quant_z(n - 1, 0, TOK)
-            for m in copies:
-                copy_x(m)
-            if n == 0:
-                quant_x(1)
-            if n == 2:
-                deal_scales(2)
-            if n == 4:
-                deal_words(3)
-            if n == 6:
-                deal_scales(3)
-            if n >= F_LAG:
-                finish(n - F_LAG)
-            for m in nxt:
-                transpose_x(m)
+        def issue_mm1(upto):
+            while issued[0] < min(upto, len(all_banks)):
+                g, h, t0, nt, lo, width = all_banks[issued[0]]
+                if not quantised[2 * g + lo // BANK]:
+                    break
+                mm1(issued[0], all_banks[issued[0]])
+                issued[0] = issued[0] + 1
 
-        for k in range(4):
-            square(last, k)
-        interleave(last - 1, 0, TOK)
-        for t in range(4):
-            affine(last, t, 0, HALF)
-        quant_z(last - 1, 0, TOK)
-        interleave(last, 0, HALF)
-        for t in range(4):
-            affine(last, t, HALF, TOK)
-        quant_z(last, 0, HALF)
-        interleave(last, HALF, TOK)
-        for m in range(last - F_LAG, last - 1):
-            mm2(m)
-            finish(m)
-        quant_z(last, HALF, TOK)
-        mm2(last - 1)
-        finish(last - 1)
-        dst = out_rows[G - 1, 1, 1]
+        def quant_block(b, slot):
+            quant_x(b // 2, BANK * (b % 2), BANK * (b % 2 + 1))
+            quantised[b] = True
+
+        issue_mm1(NY)
+        shift_scales(1)
+        load_scales(nc.sync, par_s, par_scales)
+        nc.sync.dma_start(out=par_w[:].bitcast(I32), in_=par_words.rearrange("g p n -> p g n").bitcast(I32))
+        for m in range(6, 8):
+            load_x(m)
+        shift_scales(2)
+        shift_scales(3)
+        for m in range(8, NSTEP):
+            load_x(m)
+
+
+        items = sorted([(COPY_STEP[m], ("x", m)) for m in range(2, NSTEP)] + [(FIN_STEP[m], ("o", m)) for m in range(NSTEP) if FIN_STEP[m] < 2 * NSTEP])
+
+        count = {"made": 0, "used": 0}
+        z_done = set()
+
+        def produce():
+            while count["made"] < min(count["used"] + NAUX, len(items)):
+                kind, m = items[count["made"]][1]
+                if kind == "o" and ((2 * (m // 4) + 1, m % 4) not in z_done or count["made"] >= count["used"] + LEAD_O):
+                    break
+                (transpose_x if kind == "x" else mm2)(m)
+                count["made"] = count["made"] + 1
+
+        def consume(slot):
+            for j in range(len(items)):
+                if items[j][0] == slot:
+                    kind, m = items[j][1]
+                    (copy_x if kind == "x" else finish)(m)
+                    count["used"] = count["used"] + 1
+
+        def quant_piece(g, h, lo, hi):
+            quant_z(g, h, lo, hi)
+            for q in range(lo // QUARTER, hi // QUARTER):
+                z_done.add((2 * g + h, q))
+
+        produce()
+        for i in range(len(deals)):
+            if DEAL_STEP[i] < 0:
+                deals[i][0](deals[i][1])
+        fill = []
+        for n in range(NSTEP):
+            banks, affs, done = plans[n]
+            fill.extend([(deals[i][0], (deals[i][1],)) for i in range(len(deals)) if DEAL_STEP[i] == n])
+            late = []
+            for i in range(4):
+                k = 4 * n + i
+                square(k, banks[i])
+                for args in late:
+                    affine(*args, True)
+                late = []
+                if i % 2 == 1:
+                    consume(2 * n + i // 2)
+                    for b in range(1, 2 * G):
+                        if QX_STEP[b] == 2 * n + i // 2:
+                            fill.insert(0, (quant_block, (b, 0)))
+                produce()
+                issue_mm1(k + NY + 1)
+                for args in affs[i]:
+                    if (n, i) in S_AFF:
+                        late.append(args)
+                    else:
+                        affine(*args, False)
+                    left = 4 - i
+                    if n == NSTEP - 1 and i == 2 and args == affs[i][0]:
+                        fill.extend([(interleave, (G - 1, 1, BANK, BANK + QUARTER)), (quant_piece, (G - 1, 1, BANK, BANK + QUARTER))])
+                    for r in range(-(-len(fill) // left) if affs[i] else 0):
+                        f, a = fill.pop(0)
+                        f(*a)
+                issue_mm1(k + NY + 1)
+            for args in late:
+                affine(*args, True)
+            if n == NSTEP - 1:
+                break
+            for piece in done:
+                fill.append((interleave, piece))
+            for piece in done:
+                fill.append((quant_piece, piece))
+
+        g, lo = G - 1, BANK
+        for f, a in fill:
+            f(*a)
+        interleave(g, 1, lo + QUARTER, T)
+        quant_z(g, 1, lo + QUARTER, T)
+        last = NSTEP - 1
+        for m in range(last):
+            if FIN_STEP[m] >= 2 * NSTEP:
+                mm2(m)
+                finish(m)
+        dst = out_rows[G - 1, 3]
         mm2_tile(last, 0, y_ps[0][:, 0:NP])
         mm2_tile(last, 1, y_ps[1][:, 0:NP])
-        nc.vector.tensor_copy(out=res[last][:, 0:NP], in_=y_ps[0][:, 0:NP])
-        nc.sync.dma_start(out=dst[:, 0:NP], in_=res[last][:, 0:NP])
-        nc.scalar.copy(out=res[last][:, NP : 2 * NP], in_=y_ps[1][:, 0:NP])
-        nc.scalar.dma_start(out=dst[:, NP : 2 * NP], in_=res[last][:, NP : 2 * NP])
+        nc.vector.tensor_copy(out=res[last % 8][:, 0:NP], in_=y_ps[0][:, 0:NP])
+        nc.sync.dma_start(out=dst[:, 0:NP], in_=res[last % 8][:, 0:NP])
+        nc.scalar.copy(out=res[last % 8][:, NP : 2 * NP], in_=y_ps[1][:, 0:NP])
+        nc.scalar.dma_start(out=dst[:, NP : 2 * NP], in_=res[last % 8][:, NP : 2 * NP])

@@ -18,52 +18,27 @@ ACT = mybir.ActivationFunctionType
 ALU = mybir.AluOpType
 
 P = 128
-BANK = 512
+PACK = 4
+BLOCK = 512
 QUARTER = 256
-NSTEP = 16
-NY = 5
-NAUX = 3
-WIDE = ()
-COPY_STEP = [0,0,1,2]+[2 * m - 5 for m in range(4,16)]
-QX_STEP = [0,2]+[4 * b - 3 for b in range(2,8)]
-FIN_STEP = [2 * m + 12 for m in range(16)]
-DEAL_STEP = [-1,0]
-S_AFF = ()
-SPLIT = False
+HALVES = 2 * G
+QUARTERS = 4 * G
+STEPS = 4 * G
+LAST = STEPS - 1
+Y_BANKS = 5
+SIDE_BANKS = 3
+SIDE_LEAD = 2
+X_LEAD = 5
+OUT_LAG = 10
 RUN = 4
-V_COPY = (2,)
-LEAD_O = 2
-HEADFINE = True
 
 
-def step_plan(n):
+def step_banks(n):
     g, s = divmod(n, 4)
-    if n in WIDE:
-        h, t0 = s // 2, 2 * (s % 2)
-        banks = [(g, h, t0 + e, 1, BANK * j, BANK) for e in range(2) for j in range(2)]
-        affs = [[], [(g, h, t0, 0, T)], [], [(g, h, t0 + 1, 0, T)]]
-        done = []
-        if s % 2 == 1:
-            done = [(g, h, 0, BANK), (g, h, BANK, T)] if SPLIT else [(g, h, 0, T)]
-        return banks, affs, done
-    if 4 * g in WIDE:
-        h, j = 1, s - 2
-    else:
-        j, h = divmod(s, 2)
-    lo = BANK * j
-    if n == 0:
-        banks = [(g, h, 2 * e, 2, lo + QUARTER * a, QUARTER) for a in range(2) for e in range(2)]
-        affs = [[(g, h, 2 * e + i, lo + QUARTER * a, lo + QUARTER * (a + 1)) for i in range(2)] for a in range(2) for e in range(2)]
-        if not HEADFINE:
-            affs = [[], [], [(g, h, t, lo, lo + BANK) for t in (0, 1)], [(g, h, t, lo, lo + BANK) for t in (2, 3)]]
-        return banks, affs, [(g, h, lo, lo + BANK)]
-    if n == NSTEP - 1:
-        banks = [(g, h, 2 * e, 2, lo + QUARTER * a, QUARTER) for a in range(2) for e in range(2)]
-        affs = [[(g, h, 2 * e + i, lo + QUARTER * a, lo + QUARTER * (a + 1)) for i in range(2)] for a in range(2) for e in range(2)]
-        return banks, affs, []
-    banks = [(g, h, t, 1, lo, BANK) for t in range(4)]
-    affs = [[(g, h, t, lo, lo + BANK)] for t in range(4)]
-    return banks, affs, [(g, h, lo, lo + BANK)]
+    u, lo = 2 * g + s % 2, BLOCK * (s // 2)
+    if n in (0, LAST):
+        return [(u, t, 2, lo + a, QUARTER) for a in (0, QUARTER) for t in (0, 2)]
+    return [(u, t, 1, lo, BLOCK) for t in range(PACK)]
 
 
 def tile_eeg_band_parcel_power_s14_kernel(tc, x, inv_words, inv_scales, base, ivar, par_words, par_scales, out):
@@ -73,43 +48,43 @@ def tile_eeg_band_parcel_power_s14_kernel(tc, x, inv_words, inv_scales, base, iv
         ps = ctx.enter_context(tc.psum_pool(name="ps", bufs=1))
         ctx.enter_context(tc.manual_schedule())
 
-
-        def ring(name, count, shape, dtype):
+        def tiles(name, count, shape, dtype):
             return [sb.tile(shape, dtype, name="%s%d" % (name, i), align_bytes=64) for i in range(count)]
 
         ident = sb.tile([P, P], F32, name="ident", align_bytes=64)
-        warm = sb.tile([P, 8], F32, name="warm", align_bytes=64)
+        warm_in = sb.tile([P, 8], F32, name="warm_in", align_bytes=64)
         warm_out = sb.tile([P, 8], F32, name="warm_out", align_bytes=64)
-        x_sb = ring("x", NSTEP, [P, 2 * S], BF16)
-        inv_raw = ring("invraw", G, [P, 2 * V], U8)
-        inv_w = ring("invw", G, [P, 2 * V], U8)
-        invs_raw = sb.tile([P, V], U8, name="invs_raw", align_bytes=64)
-        inv_s = ring("invs", G, [P, V], U8)
-        par_w = sb.tile([P, 2 * G, 2 * NP], U8, name="par_w", align_bytes=64)
-        par_s = sb.tile([P, 2 * G, NP], U8, name="par_s", align_bytes=64)
-        base_sb = sb.tile([P, 2 * G, 4], BF16, name="base_sb", align_bytes=64)
-        ivar_sb = sb.tile([P, 2 * G, 4], BF16, name="ivar_sb", align_bytes=64)
-        gain = sb.tile([P, 2 * G, 4], F32, name="gain", align_bytes=64)
-        shift = sb.tile([P, 2 * G, 4], F32, name="shift", align_bytes=64)
-        xg = ring("xg", 2, [P, 4 * T], BF16)
-        xq = ring("xq", G, [P, T], U32)
-        xs = ring("xs", G, [P, T], U8)
-        sq_sb = ring("sq", 3, [P, 4, T], F32)
-        z_sep = ring("zsep", 2, [P, 4, T], BF16)
-        z_int = ring("zint", 2, [P, 4 * T], BF16)
-        zq = ring("zq", 4, [P, T], U32)
-        zs = ring("zs", 4, [P, T], U8)
-        res = ring("res", 8, [P, 2 * NP], F32)
-        y_ps = [ps.tile([P, BANK], F32, name="y%d" % i) for i in range(NY)]
-        aux_ps = [ps.tile([P, BANK], F32, name="aux%d" % i) for i in range(NAUX)]
-        aux_of = {}
+        x_sb = tiles("x", QUARTERS, [P, 2 * S], BF16)
+        inv_raw = tiles("inv_raw", G, [P, 2 * V], U8)
+        inv_w = tiles("inv_w", G, [P, 2 * V], U8)
+        inv_s_raw = sb.tile([P, V], U8, name="inv_s_raw", align_bytes=64)
+        inv_s = tiles("inv_s", G, [P, V], U8)
+        par_w = sb.tile([P, HALVES, 2 * NP], U8, name="par_w", align_bytes=64)
+        par_s = sb.tile([P, HALVES, NP], U8, name="par_s", align_bytes=64)
+        rows = sb.tile([P, BLOCK], BF16, name="rows", align_bytes=64)
+        consts = sb.tile([P, 2 * HALVES * PACK], BF16, name="consts", align_bytes=64)
+        gain = sb.tile([P, PACK], F32, name="gain", align_bytes=64)
+        shift = sb.tile([P, PACK], F32, name="shift", align_bytes=64)
+        x_words = tiles("x_words", 2, [P, PACK * T], BF16)
+        xq = tiles("xq", G, [P, T], U32)
+        xs = tiles("xs", G, [P, T], U8)
+        y2 = tiles("y2", 3, [P, PACK, T], F32)
+        z_sep = tiles("z_sep", 2, [P, PACK, T], BF16)
+        z_int = tiles("z_int", 2, [P, PACK * T], BF16)
+        zq = tiles("zq", 4, [P, T], U32)
+        zs = tiles("zs", 4, [P, T], U8)
+        res = tiles("res", 8, [P, 2 * NP], F32)
+        y_ps = [ps.tile([P, BLOCK], F32, name="y%d" % i) for i in range(Y_BANKS)]
+        side_ps = [ps.tile([P, BLOCK], F32, name="side%d" % i) for i in range(SIDE_BANKS)]
 
-        def take_aux(key):
-            aux_of[key] = aux_ps[len(aux_of) % NAUX]
-            return aux_of[key]
+        x_rows = x.rearrange("g (q r i) s -> g q r (i s)", q=4, i=2)
+        out_rows = out.rearrange("g (q r i) c -> g q r (i c)", q=4, i=2)
 
-        x_rows = x.rearrange("g (q p i) s -> g q p (i s)", q=4, p=P, i=2)
-        out_rows = out.rearrange("g (q p i) c -> g q p (i c)", q=4, p=P, i=2)
+        def base_col(u, t):
+            return consts[:, PACK * u + t : PACK * u + t + 1]
+
+        def ivar_col(u, t):
+            return base_col(HALVES + u, t)
 
         def load_x(m):
             nc.sync.dma_start(out=x_sb[m][:], in_=x_rows[m // 4, m % 4])
@@ -117,60 +92,53 @@ def tile_eeg_band_parcel_power_s14_kernel(tc, x, inv_words, inv_scales, base, iv
         def load_inv(g):
             nc.sync.dma_start(out=inv_raw[g][:].bitcast(I32), in_=inv_words[g].bitcast(I32))
 
-        def load_scales(queue, plane, src):
-            for q in range(4):
-                queue.dma_start(
-                    out=plane[32 * q : 32 * q + 4, :, :].bitcast(I32),
-                    in_=src[:, 4 * q : 4 * q + 4, :].rearrange("g r n -> r g n").bitcast(I32),
-                )
+        def deal(dst, src):
+            nc.vector.tensor_copy(
+                out=dst.rearrange("p (h t m) -> p h t m", h=2, t=PACK),
+                in_=src.rearrange("p (h m t) -> p h t m", h=2, t=PACK),
+            )
 
         def deal_words(g):
-            nc.vector.tensor_copy(
-                out=inv_w[g][:].bitcast(U16).rearrange("p (h t m) -> p h t m", h=2, t=4),
-                in_=inv_raw[g][:].bitcast(U16).rearrange("p (h m t) -> p h t m", h=2, t=4),
-            )
+            deal(inv_w[g][:].bitcast(U16), inv_raw[g][:].bitcast(U16))
 
-        def deal_scales():
-            nc.vector.tensor_copy(
-                out=inv_s[0][:].rearrange("p (h t m) -> p h t m", h=2, t=4),
-                in_=invs_raw[:].rearrange("p (h m t) -> p h t m", h=2, t=4),
-            )
-
-        def shift_scales(g):
+        def move_scales(g):
             for q in range(4):
                 nc.sync.dma_start(
                     out=inv_s[g][32 * q : 32 * q + 4, :].bitcast(I32),
                     in_=inv_s[0][32 * q + 4 * g : 32 * q + 4 * g + 4, :].bitcast(I32),
                 )
 
-        def transpose_x(m):
-            words = x_sb[m][:].bitcast(F32)
-            bank = take_aux(("x", m))
-            for i in range(2):
-                for u in range(2):
-                    c = P * (2 * i + u)
-                    nc.tensor.transpose(bank[:, c : c + P], words[:, 256 * i + u : 256 * (i + 1) : 2], ident[:])
+        def transpose_words(bank, col, words):
+            for e in range(2):
+                nc.tensor.transpose(bank[:, col + P * e : col + P * (e + 1)], words[:, e : 2 * P : 2], ident[:])
 
-        def copy_x(m):
-            copy = nc.vector.tensor_copy if m in V_COPY else nc.scalar.copy
+        def transpose_x(m, bank):
+            words = x_sb[m][:].bitcast(F32)
+            for i in range(2):
+                transpose_words(bank, 2 * P * i, words[:, 2 * P * i : 2 * P * (i + 1)])
+
+        def copy_x(m, bank, copy):
             g, q = divmod(m, 4)
-            dst = xg[g % 2][:, 4 * QUARTER * q : 4 * QUARTER * (q + 1)].bitcast(F32)
+            dst = x_words[g % 2][:, PACK * QUARTER * q : PACK * QUARTER * (q + 1)].bitcast(F32)
             copy(
-                out=dst.rearrange("p (i r u) -> p i r u", i=2, u=2),
-                in_=aux_of[("x", m)][:].rearrange("p (i u r) -> p i r u", i=2, u=2),
+                out=dst.rearrange("p (i r e) -> p i r e", i=2, e=2),
+                in_=bank[:].rearrange("p (i e r) -> p i r e", i=2, e=2),
             )
 
         def quant_x(g, lo, hi):
             nc.vector.quantize_mx(
-                out=xq[g][:, lo:hi].bitcast(FP8X4), scales=xs[g][:, lo:hi], in_=xg[g % 2][:, 4 * lo : 4 * hi]
+                out=xq[g][:, lo:hi].bitcast(FP8X4), scales=xs[g][:, lo:hi], in_=x_words[g % 2][:, PACK * lo : PACK * hi]
             )
 
-        def mm1(k, bank):
-            g, h, t0, nt, lo, width = bank
-            for e in range(nt):
-                col = P * (4 * h + t0 + e)
+        banks = [bank for n in range(STEPS) for bank in step_banks(n)]
+
+        def stage1(k):
+            u, t0, count, lo, width = banks[k]
+            g, h = divmod(u, 2)
+            for e in range(count):
+                col = P * (PACK * h + t0 + e)
                 nc.tensor.matmul_mx(
-                    out=y_ps[k % NY][:, width * e : width * (e + 1)],
+                    out=y_ps[k % Y_BANKS][:, width * e : width * (e + 1)],
                     lhsT=inv_w[g][:, 2 * col : 2 * (col + P)].bitcast(FP4X4),
                     lhsT_scale=inv_s[g][:, col : col + P],
                     rhs=xq[g][:, lo : lo + width].bitcast(FP8X4),
@@ -179,47 +147,40 @@ def tile_eeg_band_parcel_power_s14_kernel(tc, x, inv_words, inv_scales, base, iv
                     stop=True,
                 )
 
-        def square(k, bank):
-            g, h, t0, nt, lo, width = bank
+        def square(k):
+            u, t0, count, lo, width = banks[k]
             nc.scalar.activation(
-                out=sq_sb[(2 * g + h) % 3][:, t0 : t0 + nt, lo : lo + width],
-                in_=y_ps[k % NY][:].rearrange("p (e c) -> p e c", e=nt),
+                out=y2[u % 3][:, t0 : t0 + count, lo : lo + width],
+                in_=y_ps[k % Y_BANKS][:].rearrange("p (e c) -> p e c", e=count),
                 func=ACT.Square,
             )
 
-        def affine(g, h, t, lo, hi, on_scalar):
-            u = 2 * g + h
-            dst, src = z_sep[u % 2][:, t, lo:hi], sq_sb[u % 3][:, t, lo:hi]
-            if on_scalar:
-                nc.scalar.activation(
-                    out=dst, in_=src, func=ACT.Identity, scale=gain[:, u, t : t + 1], bias=shift[:, u, t : t + 1]
-                )
-            else:
-                nc.vector.tensor_scalar(
-                    out=dst,
-                    in0=src,
-                    scalar1=base_sb[:, u, t : t + 1],
-                    scalar2=ivar_sb[:, u, t : t + 1],
-                    op0=ALU.subtract,
-                    op1=ALU.mult,
-                )
+        def affine(u, t, lo, hi):
+            nc.vector.tensor_scalar(
+                out=z_sep[u % 2][:, t, lo:hi],
+                in0=y2[u % 3][:, t, lo:hi],
+                scalar1=base_col(u, t),
+                scalar2=ivar_col(u, t),
+                op0=ALU.subtract,
+                op1=ALU.mult,
+            )
 
-        def interleave(g, h, lo, hi):
-            u = 2 * g + h
+        def interleave(u, lo, hi):
             nc.vector.tensor_copy(
-                out=z_int[u % 2][:, 4 * lo : 4 * hi].rearrange("p (c i t) -> p c t i", i=RUN, t=4),
+                out=z_int[u % 2][:, PACK * lo : PACK * hi].rearrange("p (c i t) -> p c t i", i=RUN, t=PACK),
                 in_=z_sep[u % 2][:, :, lo:hi].rearrange("p t (c i) -> p c t i", i=RUN),
             )
 
-        def quant_z(g, h, lo, hi):
-            u = 2 * g + h
+        def quant_z(u, lo, hi):
             nc.vector.quantize_mx(
-                out=zq[u % 4][:, lo:hi].bitcast(FP8X4), scales=zs[u % 4][:, lo:hi], in_=z_int[u % 2][:, 4 * lo : 4 * hi]
+                out=zq[u % 4][:, lo:hi].bitcast(FP8X4),
+                scales=zs[u % 4][:, lo:hi],
+                in_=z_int[u % 2][:, PACK * lo : PACK * hi],
             )
 
-        def mm2_tile(m, i, dst):
+        def stage2_rows(m, i, dst):
             g, q = divmod(m, 4)
-            cols = slice(P * (2 * q + i), P * (2 * q + i + 1))
+            cols = slice(QUARTER * q + P * i, QUARTER * q + P * (i + 1))
             for c in range(2):
                 for h in range(2):
                     u = 2 * g + h
@@ -233,35 +194,33 @@ def tile_eeg_band_parcel_power_s14_kernel(tc, x, inv_words, inv_scales, base, iv
                         stop=(h == 1),
                     )
 
-        def mm2(m):
-            bank = take_aux(("o", m))
+        def stage2(m, bank):
             for i in range(2):
-                mm2_tile(m, i, bank[:, NP * i : NP * (i + 1)])
+                stage2_rows(m, i, bank[:, NP * i : NP * (i + 1)])
 
-        def finish(m, on_vector=False):
-            if on_vector:
-                nc.vector.tensor_copy(out=res[m % 8][:], in_=aux_of[("o", m)][:])
-            else:
-                nc.scalar.copy(out=res[m % 8][:], in_=aux_of[("o", m)][:])
+        def store(m, bank):
+            nc.scalar.copy(out=res[m % 8][:], in_=bank[:])
             nc.sync.dma_start(out=out_rows[m // 4, m % 4], in_=res[m % 8][:])
 
-        nc.vector.memset(invs_raw[:].bitcast(I32), 0)
-        nc.vector.memset(warm[:], 0.0)
+        nc.vector.memset(inv_s_raw[:].bitcast(I32), 0)
+        nc.vector.memset(rows[:], 0.0)
+        nc.vector.memset(warm_in[:], 0.0)
         for g in range(1, G):
             nc.vector.memset(inv_s[g][:].bitcast(I32), 0)
-        nc.vector.memset(par_s[:].rearrange("p g n -> p (g n)").bitcast(I32), 0)
+        nc.vector.memset(par_s[:].rearrange("p u n -> p (u n)").bitcast(I32), 0)
         for q in range(4):
             nc.scalar.dma_start(
-                out=invs_raw[32 * q : 32 * q + 16, :].bitcast(I32), in_=inv_scales[:, 4 * q : 4 * q + 4, :].bitcast(I32)
+                out=inv_s_raw[32 * q : 32 * q + 16, :].bitcast(I32), in_=inv_scales[:, 4 * q : 4 * q + 4, :].bitcast(I32)
             )
-        nc.scalar.activation(out=warm_out[:], in_=warm[:], func=ACT.Square)
+        nc.scalar.activation(out=warm_out[:], in_=warm_in[:], func=ACT.Square)
         make_identity(nc, ident[:])
+
         load_x(0)
         load_inv(0)
         load_x(1)
         load_inv(1)
-        nc.sync.dma_start(out=base_sb[:], in_=base.rearrange("g (h p t) -> p (g h) t", h=2, t=4))
-        nc.sync.dma_start(out=ivar_sb[:], in_=ivar.rearrange("g (h p t) -> p (g h) t", h=2, t=4))
+        nc.sync.dma_start(out=rows[0:HALVES, :], in_=base.rearrange("g (h k) -> (g h) k", h=2))
+        nc.sync.dma_start(out=rows[HALVES : 2 * HALVES, :], in_=ivar.rearrange("g (h k) -> (g h) k", h=2))
         load_x(2)
         load_inv(2)
         load_x(3)
@@ -269,128 +228,129 @@ def tile_eeg_band_parcel_power_s14_kernel(tc, x, inv_words, inv_scales, base, iv
         load_x(4)
         load_x(5)
 
-        plans = [step_plan(n) for n in range(NSTEP)]
-        all_banks = [bank for plan in plans for bank in plan[0]]
-        deals = [(deal_words, g) for g in range(2, G)]
-
-        transpose_x(0)
-        transpose_x(1)
-        copy_x(0)
-        copy_x(1)
+        transpose_x(0, side_ps[0])
+        transpose_x(1, side_ps[1])
+        transpose_words(side_ps[2], 0, rows[:].bitcast(F32))
+        copy_x(0, side_ps[0], nc.scalar.copy)
+        copy_x(1, side_ps[1], nc.scalar.copy)
         deal_words(0)
-        deal_scales()
+        deal(inv_s[0][:], inv_s_raw[:])
         quant_x(0, 0, QUARTER)
         deal_words(1)
-        quant_x(0, QUARTER, BANK)
-        quantised = [True] + [False] * (2 * G - 1)
-        issued = [0]
+        quant_x(0, QUARTER, BLOCK)
+        nc.vector.tensor_copy(
+            out=consts[:].bitcast(F32).rearrange("p (r e) -> p r e", e=2),
+            in_=side_ps[2][:, 0 : 2 * P].rearrange("p (e r) -> p r e", e=2)[:, 0 : 2 * HALVES, :],
+        )
+        for k in range(Y_BANKS):
+            stage1(k)
+        deal_words(2)
+        last_base = consts[:, PACK * (HALVES - 1) : PACK * HALVES]
+        last_ivar = consts[:, PACK * (2 * HALVES - 1) : PACK * 2 * HALVES]
+        nc.vector.tensor_copy(out=gain[:], in_=last_ivar)
+        nc.vector.scalar_tensor_tensor(
+            out=shift[:], in0=last_base, scalar=-1.0, in1=last_ivar, op0=ALU.mult, op1=ALU.mult
+        )
 
-        def issue_mm1(upto):
-            while issued[0] < min(upto, len(all_banks)):
-                g, h, t0, nt, lo, width = all_banks[issued[0]]
-                if not quantised[2 * g + lo // BANK]:
-                    break
-                mm1(issued[0], all_banks[issued[0]])
-                issued[0] = issued[0] + 1
-
-        def quant_block(b, slot):
-            quant_x(b // 2, BANK * (b % 2), BANK * (b % 2 + 1))
-            quantised[b] = True
-
-        issue_mm1(NY)
-        shift_scales(1)
-        load_scales(nc.sync, par_s, par_scales)
-        nc.sync.dma_start(out=par_w[:].bitcast(I32), in_=par_words.rearrange("g p n -> p g n").bitcast(I32))
-        for m in range(6, 8):
+        move_scales(1)
+        for q in range(4):
+            nc.sync.dma_start(
+                out=par_s[32 * q : 32 * q + 4, :, :].bitcast(I32),
+                in_=par_scales[:, 4 * q : 4 * q + 4, :].rearrange("u r n -> r u n").bitcast(I32),
+            )
+        nc.sync.dma_start(out=par_w[:].bitcast(I32), in_=par_words.rearrange("u p n -> p u n").bitcast(I32))
+        load_x(6)
+        load_x(7)
+        move_scales(2)
+        move_scales(3)
+        for m in range(8, QUARTERS):
             load_x(m)
-        shift_scales(2)
-        shift_scales(3)
-        for m in range(8, NSTEP):
-            load_x(m)
 
+        side = sorted(
+            [(max(m - 1, 2 * m - X_LEAD), "x", m) for m in range(2, QUARTERS)]
+            + [(2 * m + OUT_LAG, "out", m) for m in range(QUARTERS - 1)]
+        )
+        in_loop = [job for job in side if job[0] < 2 * LAST]
 
-        items = sorted([(COPY_STEP[m], ("x", m)) for m in range(2, NSTEP)] + [(FIN_STEP[m], ("o", m)) for m in range(NSTEP) if FIN_STEP[m] < 2 * NSTEP])
+        def side_bank(j):
+            return side_ps[(j + 2) % SIDE_BANKS]
 
-        count = {"made": 0, "used": 0}
-        z_done = set()
+        def fill_side(j):
+            slot, kind, m = side[j]
+            (transpose_x if kind == "x" else stage2)(m, side_bank(j))
 
-        def produce():
-            while count["made"] < min(count["used"] + NAUX, len(items)):
-                kind, m = items[count["made"]][1]
-                if kind == "o" and ((2 * (m // 4) + 1, m % 4) not in z_done or count["made"] >= count["used"] + LEAD_O):
-                    break
-                (transpose_x if kind == "x" else mm2)(m)
-                count["made"] = count["made"] + 1
-
-        def consume(slot):
-            for j in range(len(items)):
-                if items[j][0] == slot:
-                    kind, m = items[j][1]
-                    (copy_x if kind == "x" else finish)(m)
-                    count["used"] = count["used"] + 1
-
-        def quant_piece(g, h, lo, hi):
-            quant_z(g, h, lo, hi)
-            for q in range(lo // QUARTER, hi // QUARTER):
-                z_done.add((2 * g + h, q))
-
-        produce()
-        for i in range(len(deals)):
-            if DEAL_STEP[i] < 0:
-                deals[i][0](deals[i][1])
-        fill = []
-        for n in range(NSTEP):
-            banks, affs, done = plans[n]
-            fill.extend([(deals[i][0], (deals[i][1],)) for i in range(len(deals)) if DEAL_STEP[i] == n])
-            late = []
-            for i in range(4):
-                k = 4 * n + i
-                square(k, banks[i])
-                for args in late:
-                    affine(*args, True)
-                late = []
-                if i % 2 == 1:
-                    consume(2 * n + i // 2)
-                    for b in range(1, 2 * G):
-                        if QX_STEP[b] == 2 * n + i // 2:
-                            fill.insert(0, (quant_block, (b, 0)))
-                produce()
-                issue_mm1(k + NY + 1)
-                for args in affs[i]:
-                    if (n, i) in S_AFF:
-                        late.append(args)
+        fill_side(0)
+        filled, emptied, issued, x_blocks = 1, 0, Y_BANKS, 1
+        for n in range(LAST):
+            if n == 0:
+                between = [(deal_words, (G - 1,))]
+            else:
+                u, t0, count, lo, width = banks[4 * n - 4]
+                between = [(interleave, (u, lo, lo + BLOCK)), (quant_z, (u, lo, lo + BLOCK))]
+            for k in range(4 * n, 4 * n + 4):
+                square(k)
+                while k % 2 == 1 and emptied < len(in_loop) and side[emptied][0] == k // 2:
+                    slot, kind, m = side[emptied]
+                    if kind == "out":
+                        store(m, side_bank(emptied))
                     else:
-                        affine(*args, False)
-                    left = 4 - i
-                    if n == NSTEP - 1 and i == 2 and args == affs[i][0]:
-                        fill.extend([(interleave, (G - 1, 1, BANK, BANK + QUARTER)), (quant_piece, (G - 1, 1, BANK, BANK + QUARTER))])
-                    for r in range(-(-len(fill) // left) if affs[i] else 0):
-                        f, a = fill.pop(0)
-                        f(*a)
-                issue_mm1(k + NY + 1)
-            for args in late:
-                affine(*args, True)
-            if n == NSTEP - 1:
-                break
-            for piece in done:
-                fill.append((interleave, piece))
-            for piece in done:
-                fill.append((quant_piece, piece))
+                        copy_x(m, side_bank(emptied), nc.vector.tensor_copy if m == 2 else nc.scalar.copy)
+                        if m % 2 == 1:
+                            first = BLOCK * (m // 2 % 2)
+                            between.insert(0, (quant_x, (m // 4, first, first + BLOCK)))
+                    emptied = emptied + 1
+                while filled < emptied + SIDE_LEAD:
+                    fill_side(filled)
+                    filled = filled + 1
+                u, t0, count, lo, width = banks[k]
+                for t in range(t0, t0 + count):
+                    affine(u, t, lo, lo + width)
+                    if between:
+                        work, args = between.pop(0)
+                        work(*args)
+                        if work == quant_x:
+                            x_blocks = x_blocks + 1
+                while issued < min(k + 1 + Y_BANKS, 8 * x_blocks):
+                    stage1(issued)
+                    issued = issued + 1
 
-        g, lo = G - 1, BANK
-        for f, a in fill:
-            f(*a)
-        interleave(g, 1, lo + QUARTER, T)
-        quant_z(g, 1, lo + QUARTER, T)
-        last = NSTEP - 1
-        for m in range(last):
-            if FIN_STEP[m] >= 2 * NSTEP:
-                mm2(m)
-                finish(m)
-        dst = out_rows[G - 1, 3]
-        mm2_tile(last, 0, y_ps[0][:, 0:NP])
-        mm2_tile(last, 1, y_ps[1][:, 0:NP])
-        nc.vector.tensor_copy(out=res[last % 8][:, 0:NP], in_=y_ps[0][:, 0:NP])
-        nc.sync.dma_start(out=dst[:, 0:NP], in_=res[last % 8][:, 0:NP])
-        nc.scalar.copy(out=res[last % 8][:, NP : 2 * NP], in_=y_ps[1][:, 0:NP])
-        nc.scalar.dma_start(out=dst[:, NP : 2 * NP], in_=res[last % 8][:, NP : 2 * NP])
+        u, lo, mid = HALVES - 1, BLOCK, BLOCK + QUARTER
+        for k in range(4 * LAST, 4 * STEPS):
+            square(k)
+        late_banks = [side_bank(j) for j in range(emptied, emptied + SIDE_BANKS)]
+        late_banks.extend([y_ps[k % Y_BANKS] for k in range(4 * STEPS, 4 * STEPS + Y_BANKS)])
+        late = [job[2] for job in side[emptied:]]
+        for j in range(filled - emptied, len(late) - 1):
+            stage2(late[j], late_banks[j])
+        affine(u, 0, lo, mid)
+        affine(u, 1, lo, mid)
+        interleave(u - 1, lo, T)
+        affine(u, 2, lo, mid)
+        affine(u, 3, lo, mid)
+        quant_z(u - 1, lo, T)
+        interleave(u, lo, mid)
+        for t in range(PACK):
+            nc.scalar.activation(
+                out=z_sep[u % 2][:, t, mid:T],
+                in_=y2[u % 3][:, t, mid:T],
+                func=ACT.Identity,
+                scale=gain[:, t : t + 1],
+                bias=shift[:, t : t + 1],
+            )
+        quant_z(u, lo, mid)
+        stage2(late[-1], late_banks[len(late) - 1])
+        for c in (mid, mid + P):
+            interleave(u, c, c + P)
+        for c in (mid, mid + P):
+            quant_z(u, c, c + P)
+        for j in range(len(late)):
+            store(late[j], late_banks[j])
+
+        m = QUARTERS - 1
+        left, right = late_banks[len(late)], late_banks[len(late) + 1]
+        stage2_rows(m, 0, left[:, 0:NP])
+        stage2_rows(m, 1, right[:, 0:NP])
+        nc.vector.tensor_copy(out=res[m % 8][:, 0:NP], in_=left[:, 0:NP])
+        nc.sync.dma_start(out=out_rows[G - 1, 3][:, 0:NP], in_=res[m % 8][:, 0:NP])
+        nc.scalar.copy(out=res[m % 8][:, NP : 2 * NP], in_=right[:, 0:NP])
+        nc.scalar.dma_start(out=out_rows[G - 1, 3][:, NP : 2 * NP], in_=res[m % 8][:, NP : 2 * NP])

@@ -52,8 +52,6 @@ def tile_eeg_band_parcel_power_s14_kernel(tc, x, inv_words, inv_scales, base, iv
             return [sb.tile(shape, dtype, name="%s%d" % (name, i), align_bytes=64) for i in range(count)]
 
         ident = sb.tile([P, P], F32, name="ident", align_bytes=64)
-        warm_in = sb.tile([P, 8], F32, name="warm_in", align_bytes=64)
-        warm_out = sb.tile([P, 8], F32, name="warm_out", align_bytes=64)
         x_sb = tiles("x", QUARTERS, [P, 2 * S], BF16)
         inv_raw = tiles("inv_raw", G, [P, 2 * V], U8)
         inv_w = tiles("inv_w", G, [P, 2 * V], U8)
@@ -204,7 +202,6 @@ def tile_eeg_band_parcel_power_s14_kernel(tc, x, inv_words, inv_scales, base, iv
 
         nc.vector.memset(inv_s_raw[:].bitcast(I32), 0)
         nc.vector.memset(rows[:], 0.0)
-        nc.vector.memset(warm_in[:], 0.0)
         for g in range(1, G):
             nc.vector.memset(inv_s[g][:].bitcast(I32), 0)
         nc.vector.memset(par_s[:].rearrange("p u n -> p (u n)").bitcast(I32), 0)
@@ -212,7 +209,6 @@ def tile_eeg_band_parcel_power_s14_kernel(tc, x, inv_words, inv_scales, base, iv
             nc.scalar.dma_start(
                 out=inv_s_raw[32 * q : 32 * q + 16, :].bitcast(I32), in_=inv_scales[:, 4 * q : 4 * q + 4, :].bitcast(I32)
             )
-        nc.scalar.activation(out=warm_out[:], in_=warm_in[:], func=ACT.Square)
         make_identity(nc, ident[:])
 
         load_x(0)

@@ -60,8 +60,8 @@ def tile_eeg_band_parcel_power_s14_kernel(tc, x, inv_words, inv_scales, base, iv
         par_w = sb.tile([P, HALVES, 2 * NP], U8, name="par_w", align_bytes=64)
         par_s = sb.tile([P, HALVES, NP], U8, name="par_s", align_bytes=64)
         rows = sb.tile([P, BLOCK], BF16, name="rows", align_bytes=64)
-        consts = sb.tile([P, 2 * HALVES * PACK], BF16, name="consts", align_bytes=64)
-        gain = sb.tile([P, PACK], F32, name="gain", align_bytes=64)
+        cols16 = sb.tile([P, 2 * HALVES * PACK], BF16, name="cols16", align_bytes=64)
+        consts = sb.tile([P, 2 * HALVES * PACK], F32, name="consts", align_bytes=64)
         shift = sb.tile([P, PACK], F32, name="shift", align_bytes=64)
         x_words = tiles("x_words", 2, [P, PACK * T], BF16)
         xq = tiles("xq", G, [P, T], U32)
@@ -176,25 +176,25 @@ def tile_eeg_band_parcel_power_s14_kernel(tc, x, inv_words, inv_scales, base, iv
                 in_=z_int[u % 2][:, PACK * lo : PACK * hi],
             )
 
-        def stage2_rows(m, i, dst):
+        def stage2_pass(m, i, c, h, dst):
             g, q = divmod(m, 4)
+            u = 2 * g + h
             cols = slice(QUARTER * q + P * i, QUARTER * q + P * (i + 1))
-            for c in range(2):
-                for h in range(2):
-                    u = 2 * g + h
-                    nc.tensor.matmul_mx(
-                        out=dst[:, P * c : P * (c + 1)],
-                        lhsT=zq[u % 4][:, cols].bitcast(FP8X4),
-                        lhsT_scale=zs[u % 4][:, cols],
-                        rhs=par_w[:, u, 2 * P * c : 2 * P * (c + 1)].bitcast(FP4X4),
-                        rhs_scale=par_s[:, u, P * c : P * (c + 1)],
-                        start=(h == 0),
-                        stop=(h == 1),
-                    )
+            nc.tensor.matmul_mx(
+                out=dst,
+                lhsT=zq[u % 4][:, cols].bitcast(FP8X4),
+                lhsT_scale=zs[u % 4][:, cols],
+                rhs=par_w[:, u, 2 * P * c : 2 * P * (c + 1)].bitcast(FP4X4),
+                rhs_scale=par_s[:, u, P * c : P * (c + 1)],
+                start=(h == 0),
+                stop=(h == 1),
+            )
 
         def stage2(m, bank):
             for i in range(2):
-                stage2_rows(m, i, bank[:, NP * i : NP * (i + 1)])
+                for c in range(2):
+                    for h in range(2):
+                        stage2_pass(m, i, c, h, bank[:, NP * i + P * c : NP * i + P * (c + 1)])
 
         def store(m, bank):
             nc.scalar.copy(out=res[m % 8][:], in_=bank[:])
@@ -235,15 +235,15 @@ def tile_eeg_band_parcel_power_s14_kernel(tc, x, inv_words, inv_scales, base, iv
         deal_words(1)
         quant_x(0, QUARTER, BLOCK)
         nc.vector.tensor_copy(
-            out=consts[:].bitcast(F32).rearrange("p (r e) -> p r e", e=2),
+            out=cols16[:].bitcast(F32).rearrange("p (r e) -> p r e", e=2),
             in_=side_ps[2][:, 0 : 2 * P].rearrange("p (e r) -> p r e", e=2)[:, 0 : 2 * HALVES, :],
         )
         for k in range(Y_BANKS):
             stage1(k)
         deal_words(2)
-        last_base = consts[:, PACK * (HALVES - 1) : PACK * HALVES]
-        last_ivar = consts[:, PACK * (2 * HALVES - 1) : PACK * 2 * HALVES]
-        nc.vector.tensor_copy(out=gain[:], in_=last_ivar)
+        nc.vector.tensor_copy(out=consts[:], in_=cols16[:])
+        last_base = cols16[:, PACK * (HALVES - 1) : PACK * HALVES]
+        last_ivar = cols16[:, PACK * (2 * HALVES - 1) : PACK * 2 * HALVES]
         nc.vector.scalar_tensor_tensor(
             out=shift[:], in0=last_base, scalar=-1.0, in1=last_ivar, op0=ALU.mult, op1=ALU.mult
         )
@@ -263,7 +263,7 @@ def tile_eeg_band_parcel_power_s14_kernel(tc, x, inv_words, inv_scales, base, iv
             load_x(m)
 
         side = sorted(
-            [(max(m - 1, 2 * m - X_LEAD), "x", m) for m in range(2, QUARTERS)]
+            [(max(1, 2 * m - X_LEAD), "x", m) for m in range(2, QUARTERS)]
             + [(2 * m + OUT_LAG, "out", m) for m in range(QUARTERS - 1)]
         )
         in_loop = [job for job in side if job[0] < 2 * LAST]
@@ -316,7 +316,8 @@ def tile_eeg_band_parcel_power_s14_kernel(tc, x, inv_words, inv_scales, base, iv
         late_banks = [side_bank(j) for j in range(emptied, emptied + SIDE_BANKS)]
         late_banks.extend([y_ps[k % Y_BANKS] for k in range(4 * STEPS, 4 * STEPS + Y_BANKS)])
         late = [job[2] for job in side[emptied:]]
-        for j in range(filled - emptied, len(late) - 1):
+        held = len(late) - 1
+        for j in range(filled - emptied, held):
             stage2(late[j], late_banks[j])
         affine(u, 0, lo, mid)
         affine(u, 1, lo, mid)
@@ -324,29 +325,32 @@ def tile_eeg_band_parcel_power_s14_kernel(tc, x, inv_words, inv_scales, base, iv
         affine(u, 2, lo, mid)
         affine(u, 3, lo, mid)
         quant_z(u - 1, lo, T)
+        groups = [(i, c, late_banks[held + 2 * i + c][:, 0:P]) for i in range(2) for c in range(2)]
+        for i, c, dst in groups:
+            stage2_pass(QUARTERS - 1, i, c, 0, dst)
         interleave(u, lo, mid)
         for t in range(PACK):
             nc.scalar.activation(
                 out=z_sep[u % 2][:, t, mid:T],
                 in_=y2[u % 3][:, t, mid:T],
                 func=ACT.Identity,
-                scale=gain[:, t : t + 1],
+                scale=ivar_col(u, t),
                 bias=shift[:, t : t + 1],
             )
         quant_z(u, lo, mid)
-        stage2(late[-1], late_banks[len(late) - 1])
+        store(late[0], late_banks[0])
+        stage2(late[held], late_banks[0])
         for c in (mid, mid + P):
             interleave(u, c, c + P)
         for c in (mid, mid + P):
             quant_z(u, c, c + P)
-        for j in range(len(late)):
-            store(late[j], late_banks[j])
+        for j in range(1, len(late)):
+            store(late[j], late_banks[j % held])
 
         m = QUARTERS - 1
-        left, right = late_banks[len(late)], late_banks[len(late) + 1]
-        stage2_rows(m, 0, left[:, 0:NP])
-        stage2_rows(m, 1, right[:, 0:NP])
-        nc.vector.tensor_copy(out=res[m % 8][:, 0:NP], in_=left[:, 0:NP])
-        nc.sync.dma_start(out=out_rows[G - 1, 3][:, 0:NP], in_=res[m % 8][:, 0:NP])
-        nc.scalar.copy(out=res[m % 8][:, NP : 2 * NP], in_=right[:, 0:NP])
-        nc.scalar.dma_start(out=out_rows[G - 1, 3][:, NP : 2 * NP], in_=res[m % 8][:, NP : 2 * NP])
+        for i, c, dst in groups:
+            stage2_pass(m, i, c, 1, dst)
+        for i, copy, queue in ((0, nc.vector.tensor_copy, nc.sync), (1, nc.scalar.copy, nc.scalar)):
+            for c in range(2):
+                copy(out=res[m % 8][:, NP * i + P * c : NP * i + P * (c + 1)], in_=groups[2 * i + c][2])
+            queue.dma_start(out=out_rows[G - 1, 3][:, NP * i : NP * (i + 1)], in_=res[m % 8][:, NP * i : NP * (i + 1)])

from contextlib import ExitStack

import concourse.mybir as mybir
from concourse.masks import make_identity

G, T, S, V, NP = 4, 1024, 512, 1024, 256
FLOPS = 2 * G * T * S * V + 2 * G * T * V * NP

F32 = mybir.dt.float32
BF16 = mybir.dt.bfloat16
I32 = mybir.dt.int32
U32 = mybir.dt.uint32
U16 = mybir.dt.uint16
U8 = mybir.dt.uint8
FP8X4 = mybir.dt.float8_e4m3fn_x4
FP4X4 = mybir.dt.float4_e2m1fn_x4
ACT = mybir.ActivationFunctionType
ALU = mybir.AluOpType

P = 128
PACK = 4
BLOCK = 512
QUARTER = 256
HALVES = 2 * G
QUARTERS = 4 * G
STEPS = 4 * G
LAST = STEPS - 1
Y_BANKS = 5
SIDE_BANKS = 3
SIDE_LEAD = 2
X_LEAD = 5
OUT_LAG = 10
RUN = 4


def step_banks(n):
    g, s = divmod(n, 4)
    u, lo = 2 * g + s % 2, BLOCK * (s // 2)
    if n in (0, LAST):
        return [(u, t, 2, lo + a, QUARTER) for a in (0, QUARTER) for t in (0, 2)]
    return [(u, t, 1, lo, BLOCK) for t in range(PACK)]


def tile_eeg_band_parcel_power_s14_kernel(tc, x, inv_words, inv_scales, base, ivar, par_words, par_scales, out):
    nc = tc.nc
    with ExitStack() as ctx:
        sb = ctx.enter_context(tc.tile_pool(name="sb", bufs=1))
        ps = ctx.enter_context(tc.psum_pool(name="ps", bufs=1))
        ctx.enter_context(tc.manual_schedule())

        def tiles(name, count, shape, dtype):
            return [sb.tile(shape, dtype, name="%s%d" % (name, i), align_bytes=64) for i in range(count)]

        ident = sb.tile([P, P], F32, name="ident", align_bytes=64)
        x_sb = tiles("x", QUARTERS, [P, 2 * S], BF16)
        inv_raw = tiles("inv_raw", G, [P, 2 * V], U8)
        inv_w = tiles("inv_w", G, [P, 2 * V], U8)
        inv_s_raw = sb.tile([P, V], U8, name="inv_s_raw", align_bytes=64)
        inv_s = tiles("inv_s", G, [P, V], U8)
        par_w = sb.tile([P, HALVES, 2 * NP], U8, name="par_w", align_bytes=64)
        par_s = sb.tile([P, HALVES, NP], U8, name="par_s", align_bytes=64)
        rows = sb.tile([P, BLOCK], BF16, name="rows", align_bytes=64)
        cols16 = sb.tile([P, 2 * HALVES * PACK], BF16, name="cols16", align_bytes=64)
        consts = sb.tile([P, 2 * HALVES * PACK], F32, name="consts", align_bytes=64)
        shift = sb.tile([P, PACK], F32, name="shift", align_bytes=64)
        x_words = tiles("x_words", 2, [P, PACK * T], BF16)
        xq = tiles("xq", G, [P, T], U32)
        xs = tiles("xs", G, [P, T], U8)
        y2 = tiles("y2", 3, [P, PACK, T], F32)
        z_sep = tiles("z_sep", 2, [P, PACK, T], BF16)
        z_int = tiles("z_int", 2, [P, PACK * T], BF16)
        zq = tiles("zq", 4, [P, T], U32)
        zs = tiles("zs", 4, [P, T], U8)
        res = tiles("res", 8, [P, 2 * NP], F32)
        y_ps = [ps.tile([P, BLOCK], F32, name="y%d" % i) for i in range(Y_BANKS)]
        side_ps = [ps.tile([P, BLOCK], F32, name="side%d" % i) for i in range(SIDE_BANKS)]

        x_rows = x.rearrange("g (q r i) s -> g q r (i s)", q=4, i=2)
        out_rows = out.rearrange("g (q r i) c -> g q r (i c)", q=4, i=2)

        def base_col(u, t):
            return consts[:, PACK * u + t : PACK * u + t + 1]

        def ivar_col(u, t):
            return base_col(HALVES + u, t)

        def load_x(m):
            nc.sync.dma_start(out=x_sb[m][:], in_=x_rows[m // 4, m % 4])

        def load_inv(g):
            nc.sync.dma_start(out=inv_raw[g][:].bitcast(I32), in_=inv_words[g].bitcast(I32))

        def deal(dst, src):
            nc.vector.tensor_copy(
                out=dst.rearrange("p (h t m) -> p h t m", h=2, t=PACK),
                in_=src.rearrange("p (h m t) -> p h t m", h=2, t=PACK),
            )

        def deal_words(g):
            deal(inv_w[g][:].bitcast(U16), inv_raw[g][:].bitcast(U16))

        def move_scales(g):
            for q in range(4):
                nc.sync.dma_start(
                    out=inv_s[g][32 * q : 32 * q + 4, :].bitcast(I32),
                    in_=inv_s[0][32 * q + 4 * g : 32 * q + 4 * g + 4, :].bitcast(I32),
                )

        def transpose_words(bank, col, words):
            for e in range(2):
                nc.tensor.transpose(bank[:, col + P * e : col + P * (e + 1)], words[:, e : 2 * P : 2], ident[:])

        def transpose_x(m, bank):
            words = x_sb[m][:].bitcast(F32)
            for i in range(2):
                transpose_words(bank, 2 * P * i, words[:, 2 * P * i : 2 * P * (i + 1)])

        def copy_x(m, bank, copy):
            g, q = divmod(m, 4)
            dst = x_words[g % 2][:, PACK * QUARTER * q : PACK * QUARTER * (q + 1)].bitcast(F32)
            copy(
                out=dst.rearrange("p (i r e) -> p i r e", i=2, e=2),
                in_=bank[:].rearrange("p (i e r) -> p i r e", i=2, e=2),
            )

        def quant_x(g, lo, hi):
            nc.vector.quantize_mx(
                out=xq[g][:, lo:hi].bitcast(FP8X4), scales=xs[g][:, lo:hi], in_=x_words[g % 2][:, PACK * lo : PACK * hi]
            )

        banks = [bank for n in range(STEPS) for bank in step_banks(n)]

        def stage1(k):
            u, t0, count, lo, width = banks[k]
            g, h = divmod(u, 2)
            for e in range(count):
                col = P * (PACK * h + t0 + e)
                nc.tensor.matmul_mx(
                    out=y_ps[k % Y_BANKS][:, width * e : width * (e + 1)],
                    lhsT=inv_w[g][:, 2 * col : 2 * (col + P)].bitcast(FP4X4),
                    lhsT_scale=inv_s[g][:, col : col + P],
                    rhs=xq[g][:, lo : lo + width].bitcast(FP8X4),
                    rhs_scale=xs[g][:, lo : lo + width],
                    start=True,
                    stop=True,
                )

        def square(k):
            u, t0, count, lo, width = banks[k]
            nc.scalar.activation(
                out=y2[u % 3][:, t0 : t0 + count, lo : lo + width],
                in_=y_ps[k % Y_BANKS][:].rearrange("p (e c) -> p e c", e=count),
                func=ACT.Square,
            )

        def affine(u, t, lo, hi):
            nc.vector.tensor_scalar(
                out=z_sep[u % 2][:, t, lo:hi],
                in0=y2[u % 3][:, t, lo:hi],
                scalar1=base_col(u, t),
                scalar2=ivar_col(u, t),
                op0=ALU.subtract,
                op1=ALU.mult,
            )

        def interleave(u, lo, hi):
            nc.vector.tensor_copy(
                out=z_int[u % 2][:, PACK * lo : PACK * hi].rearrange("p (c i t) -> p c t i", i=RUN, t=PACK),
                in_=z_sep[u % 2][:, :, lo:hi].rearrange("p t (c i) -> p c t i", i=RUN),
            )

        def quant_z(u, lo, hi):
            nc.vector.quantize_mx(
                out=zq[u % 4][:, lo:hi].bitcast(FP8X4),
                scales=zs[u % 4][:, lo:hi],
                in_=z_int[u % 2][:, PACK * lo : PACK * hi],
            )

        def stage2_pass(m, i, c, h, dst):
            g, q = divmod(m, 4)
            u = 2 * g + h
            cols = slice(QUARTER * q + P * i, QUARTER * q + P * (i + 1))
            nc.tensor.matmul_mx(
                out=dst,
                lhsT=zq[u % 4][:, cols].bitcast(FP8X4),
                lhsT_scale=zs[u % 4][:, cols],
                rhs=par_w[:, u, 2 * P * c : 2 * P * (c + 1)].bitcast(FP4X4),
                rhs_scale=par_s[:, u, P * c : P * (c + 1)],
                start=(h == 0),
                stop=(h == 1),
            )

        def stage2(m, bank):
            for i in range(2):
                for c in range(2):
                    for h in range(2):
                        stage2_pass(m, i, c, h, bank[:, NP * i + P * c : NP * i + P * (c + 1)])

        def store(m, bank):
            nc.scalar.copy(out=res[m % 8][:], in_=bank[:])
            nc.sync.dma_start(out=out_rows[m // 4, m % 4], in_=res[m % 8][:])

        nc.vector.memset(inv_s_raw[:].bitcast(I32), 0)
        nc.vector.memset(rows[:], 0.0)
        for g in range(1, G):
            nc.vector.memset(inv_s[g][:].bitcast(I32), 0)
        nc.vector.memset(par_s[:].rearrange("p u n -> p (u n)").bitcast(I32), 0)
        for q in range(4):
            nc.scalar.dma_start(
                out=inv_s_raw[32 * q : 32 * q + 16, :].bitcast(I32), in_=inv_scales[:, 4 * q : 4 * q + 4, :].bitcast(I32)
            )
        make_identity(nc, ident[:])

        load_x(0)
        load_inv(0)
        load_x(1)
        load_inv(1)
        nc.sync.dma_start(out=rows[0:HALVES, :], in_=base.rearrange("g (h k) -> (g h) k", h=2))
        nc.sync.dma_start(out=rows[HALVES : 2 * HALVES, :], in_=ivar.rearrange("g (h k) -> (g h) k", h=2))
        load_x(2)
        load_inv(2)
        load_x(3)
        load_inv(3)
        load_x(4)
        load_x(5)

        transpose_x(0, side_ps[0])
        transpose_x(1, side_ps[1])
        transpose_words(side_ps[2], 0, rows[:].bitcast(F32))
        copy_x(0, side_ps[0], nc.scalar.copy)
        copy_x(1, side_ps[1], nc.scalar.copy)
        deal_words(0)
        deal(inv_s[0][:], inv_s_raw[:])
        quant_x(0, 0, QUARTER)
        deal_words(1)
        quant_x(0, QUARTER, BLOCK)
        nc.vector.tensor_copy(
            out=cols16[:].bitcast(F32).rearrange("p (r e) -> p r e", e=2),
            in_=side_ps[2][:, 0 : 2 * P].rearrange("p (e r) -> p r e", e=2)[:, 0 : 2 * HALVES, :],
        )
        for k in range(Y_BANKS):
            stage1(k)
        deal_words(2)
        nc.vector.tensor_copy(out=consts[:], in_=cols16[:])
        last_base = cols16[:, PACK * (HALVES - 1) : PACK * HALVES]
        last_ivar = cols16[:, PACK * (2 * HALVES - 1) : PACK * 2 * HALVES]
        nc.vector.scalar_tensor_tensor(
            out=shift[:], in0=last_base, scalar=-1.0, in1=last_ivar, op0=ALU.mult, op1=ALU.mult
        )

        move_scales(1)
        for q in range(4):
            nc.sync.dma_start(
                out=par_s[32 * q : 32 * q + 4, :, :].bitcast(I32),
                in_=par_scales[:, 4 * q : 4 * q + 4, :].rearrange("u r n -> r u n").bitcast(I32),
            )
        nc.sync.dma_start(out=par_w[:].bitcast(I32), in_=par_words.rearrange("u p n -> p u n").bitcast(I32))
        load_x(6)
        load_x(7)
        move_scales(2)
        move_scales(3)
        for m in range(8, QUARTERS):
            load_x(m)

        side = sorted(
            [(max(1, 2 * m - X_LEAD), "x", m) for m in range(2, QUARTERS)]
            + [(2 * m + OUT_LAG, "out", m) for m in range(QUARTERS - 1)]
        )
        in_loop = [job for job in side if job[0] < 2 * LAST]

        def side_bank(j):
            return side_ps[(j + 2) % SIDE_BANKS]

        def fill_side(j):
            slot, kind, m = side[j]
            (transpose_x if kind == "x" else stage2)(m, side_bank(j))

        fill_side(0)
        filled, emptied, issued, x_blocks = 1, 0, Y_BANKS, 1
        for n in range(LAST):
            if n == 0:
                between = [(deal_words, (G - 1,))]
            else:
                u, t0, count, lo, width = banks[4 * n - 4]
                between = [(interleave, (u, lo, lo + BLOCK)), (quant_z, (u, lo, lo + BLOCK))]
            for k in range(4 * n, 4 * n + 4):
                square(k)
                while k % 2 == 1 and emptied < len(in_loop) and side[emptied][0] == k // 2:
                    slot, kind, m = side[emptied]
                    if kind == "out":
                        store(m, side_bank(emptied))
                    else:
                        copy_x(m, side_bank(emptied), nc.vector.tensor_copy if m == 2 else nc.scalar.copy)
                        if m % 2 == 1:
                            first = BLOCK * (m // 2 % 2)
                            between.insert(0, (quant_x, (m // 4, first, first + BLOCK)))
                    emptied = emptied + 1
                while filled < emptied + SIDE_LEAD:
                    fill_side(filled)
                    filled = filled + 1
                u, t0, count, lo, width = banks[k]
                for t in range(t0, t0 + count):
                    affine(u, t, lo, lo + width)
                    if between:
                        work, args = between.pop(0)
                        work(*args)
                        if work == quant_x:
                            x_blocks = x_blocks + 1
                while issued < min(k + 1 + Y_BANKS, 8 * x_blocks):
                    stage1(issued)
                    issued = issued + 1

        u, lo, mid = HALVES - 1, BLOCK, BLOCK + QUARTER
        for k in range(4 * LAST, 4 * STEPS):
            square(k)
        late_banks = [side_bank(j) for j in range(emptied, emptied + SIDE_BANKS)]
        late_banks.extend([y_ps[k % Y_BANKS] for k in range(4 * STEPS, 4 * STEPS + Y_BANKS)])
        late = [job[2] for job in side[emptied:]]
        held = len(late) - 1
        for j in range(filled - emptied, held):
            stage2(late[j], late_banks[j])
        affine(u, 0, lo, mid)
        affine(u, 1, lo, mid)
        interleave(u - 1, lo, T)
        affine(u, 2, lo, mid)
        affine(u, 3, lo, mid)
        quant_z(u - 1, lo, T)
        groups = [(i, c, late_banks[held + 2 * i + c][:, 0:P]) for i in range(2) for c in range(2)]
        for i, c, dst in groups:
            stage2_pass(QUARTERS - 1, i, c, 0, dst)
        interleave(u, lo, mid)
        for t in range(PACK):
            nc.scalar.activation(
                out=z_sep[u % 2][:, t, mid:T],
                in_=y2[u % 3][:, t, mid:T],
                func=ACT.Identity,
                scale=ivar_col(u, t),
                bias=shift[:, t : t + 1],
            )
        quant_z(u, lo, mid)
        store(late[0], late_banks[0])
        stage2(late[held], late_banks[0])
        for c in (mid, mid + P):
            interleave(u, c, c + P)
        for c in (mid, mid + P):
            quant_z(u, c, c + P)
        for j in range(1, len(late)):
            store(late[j], late_banks[j % held])

        m = QUARTERS - 1
        for i, c, dst in groups:
            stage2_pass(m, i, c, 1, dst)
        for i, copy, queue in ((0, nc.vector.tensor_copy, nc.sync), (1, nc.scalar.copy, nc.scalar)):
            for c in range(2):
                copy(out=res[m % 8][:, NP * i + P * c : NP * i + P * (c + 1)], in_=groups[2 * i + c][2])
            queue.dma_start(out=out_rows[G - 1, 3][:, NP * i : NP * (i + 1)], in_=res[m % 8][:, NP * i : NP * (i + 1)])
